import numpy as np
import ml_dtypes


def mxq(x, axis, fmt="e4m3"):
    dtype, down = {"e4m3": (ml_dtypes.float8_e4m3fn, 7), "e5m2": (ml_dtypes.float8_e5m2, 14)}[fmt]
    v = np.moveaxis(np.asarray(x, np.float32).astype(ml_dtypes.bfloat16).astype(np.float64), axis, -1)
    blocks = v.reshape(v.shape[:-1] + (-1, 32))
    amax = np.abs(blocks).max(-1, keepdims=True)
    byte = np.maximum(np.where(amax > 0, np.frexp(amax)[1] - 1 + 127, 0) - down, 1)
    scale = np.exp2(byte - 127.0)
    codes = (blocks / scale).astype(np.float32).astype(dtype).astype(np.float64)
    return np.moveaxis((codes * scale).reshape(v.shape), -1, axis)


WIDE = False


def mx_kscale(k):
    if not WIDE:
        return np.ones(k)
    levels = np.array([10, -10, 5, -5, 0])
    if k % 512:
        return np.exp2(np.random.permutation(np.resize(levels, k // 32))).repeat(32)
    a = np.empty((k // 512, 16))
    for p in range(k // 512):
        a[p, :8] = np.random.permutation(np.resize(levels, 8))
        for g in range(8):
            far = levels[np.abs(levels - a[p, g]) >= 10]
            a[p, g + 8] = far[np.random.randint(len(far))]
    return np.exp2(a.ravel()).repeat(32)


def f64(x):
    return np.asarray(x).astype(np.float64)


def striped(idx):
    return np.tile(idx.reshape(-1, 16).T, (8, 1)).astype(np.uint16)


def unstriped(offs):
    return offs[:16].T.reshape(-1).astype(np.int64)


def pack_weight(w):
    k, n = w.shape
    w = f64(np.asarray(w, np.float32).astype(ml_dtypes.bfloat16)).reshape(k // 32, 32, n)
    amax = np.abs(w).max(1)
    byte = np.clip(np.where(amax > 0, np.frexp(amax)[1] - 1 + 127 - 7, 1), 1, 254)
    scaled = (w * np.exp2(127.0 - byte)[:, None, :]).reshape(k, n).astype(np.float32)
    words = np.ascontiguousarray(scaled.reshape(k // 512, 128, 4, n).transpose(0, 1, 3, 2)).astype(ml_dtypes.float8_e4m3fn).view(np.uint8)
    return words, np.ascontiguousarray(byte.astype(np.uint8).reshape(k // 512, 16, n))


def unpack_weight(words, scales):
    g, p, n, _ = words.shape
    vals = np.ascontiguousarray(words).view(ml_dtypes.float8_e4m3fn).astype(np.float64) * np.repeat(np.exp2(scales.astype(np.float64) - 127.0), 8, axis=1)[..., None]
    return vals.transpose(0, 1, 3, 2).reshape(g * 512, n)


K, T, S, H, N = 512, 4096, 1024, 512, 256
P = 2 ** 7


def setup_inputs():
    n = np.random.standard_normal
    s = mx_kscale(K)[:, None]
    u = mx_kscale(H)
    packed_xT = pack_weight(n((K, T)) * s)
    return {
        "x_words": packed_xT[0],
        "x_scales": packed_xT[1],
        "w1": (n((K, H)) / np.sqrt(K) / s * u).astype(np.float32),
        "w2": (n((H, N)) / np.sqrt(H) / u[:, None]).astype(np.float32),
        "score": (np.tile(n(T), (P, 1))).astype(np.float32),
        "offs": striped(np.random.permutation(T)[:S]),
    }


def reference(x_words, x_scales, w1, w2, score, offs):
    xq = unpack_weight(x_words, x_scales)[:, unstriped(offs)]
    y = mxq(f64(w1), 0, "e4m3").T @ xq
    sc = f64(score)[:1][:, unstriped(offs)]
    ee = np.exp(sc)
    p = y * ee
    total = ee.sum(axis=1, keepdims=True)
    ctx = p.sum(axis=1, keepdims=True) / total
    z = y + ctx
    return mxq(f64(w2), 0, "e4m3").T @ mxq(z, 0, "e4m3")

@@ -1,0 +1,205 @@
+from contextlib import ExitStack
+
+import concourse.mybir as mybir
+from concourse.masks import make_identity
+
+K, T, S, H, N = 512, 4096, 1024, 512, 256
+P = 128
+PACK = 4
+BANK = 512
+FLOPS = 2 * K * H * S + 2 * H * N * S
+BYTES = T * P * 4 + 16 * T + 4 * K * H + 4 * H * N + 4 * T + 2 * P * (S // 16) + 4 * N * S
+
+F32 = mybir.dt.float32
+BF16 = mybir.dt.bfloat16
+I32 = mybir.dt.int32
+U32 = mybir.dt.uint32
+U16 = mybir.dt.uint16
+U8 = mybir.dt.uint8
+FP8X4 = mybir.dt.float8_e4m3fn_x4
+ALU = mybir.AluOpType
+ACT = mybir.ActivationFunctionType
+AXIS = mybir.AxisListType
+
+SCORE_ROW = P - 1
+ZERO_FIRST = 128
+ZERO_SPLIT = 2560
+PIECES = (256, 256, 256, 128, 128)
+
+
+def tile_picked_ygcb_none_p_kernel(tc, x_words, x_scales, w1, w2, score, offs, out):
+    nc = tc.nc
+    halves = S // BANK
+    blocks = S // P
+    with ExitStack() as ctx:
+        keep = ctx.enter_context(tc.tile_pool(name="keep", bufs=1))
+        psum = ctx.enter_context(tc.psum_pool(name="psum", bufs=1))
+
+        def bank(b, name):
+            return psum.tile([P, BANK], F32, name=name, tag="bank%d" % b)
+
+        offsets = keep.tile([P, S // 16], U16, name="offsets")
+        nc.sync.dma_start(offsets[:], offs)
+        score_table = keep.tile([P, T], F32, name="score_table", tag="score_table", align_bytes=64)
+        nc.sync.dma_start(score_table[SCORE_ROW:P, :], score[0:1, :])
+        w1_raw = keep.tile([P, PACK, H], F32, name="w1_raw", tag="raw")
+        nc.sync.dma_start(w1_raw[:], w1.rearrange("(p j) c -> p j c", j=PACK))
+        scale_table = keep.tile([P, T // 4], I32, name="scale_table", tag="scale_table", align_bytes=64)
+        nc.vector.memset(scale_table[:], 0)
+        zero = keep.tile([P, 1], F32, name="zero", tag="word_table", align_bytes=64)
+        nc.gpsimd.memset(zero[:], 0.0)
+        zero_s = keep.tile([P, 1], F32, name="zero_s")
+        nc.gpsimd.memset(zero_s[:], 0.0)
+        nc.vector.tensor_copy(score_table[0:SCORE_ROW, 0:ZERO_FIRST], zero[0:SCORE_ROW, :].to_broadcast([SCORE_ROW, ZERO_FIRST]))
+        nc.vector.memset(score_table[0:SCORE_ROW, ZERO_FIRST:ZERO_SPLIT], 0.0)
+        for q in range(4):
+            nc.sync.dma_start(scale_table[32 * q : 32 * q + 4, :], x_scales[0, 4 * q : 4 * q + 4, :].bitcast(I32))
+        nc.scalar.copy(score_table[0:SCORE_ROW, ZERO_SPLIT:T], zero_s[0:SCORE_ROW, :].to_broadcast([SCORE_ROW, T - ZERO_SPLIT]))
+        word_table = keep.tile([P, T], U32, name="word_table", tag="word_table", align_bytes=64)
+        nc.sync.dma_start(word_table[:].bitcast(I32), x_words[0].rearrange("p n t -> p (n t)").bitcast(I32))
+
+        ident = keep.tile([P, P], F32, name="ident")
+        make_identity(nc, ident[:])
+        warm = keep.tile([P, 1], F32, name="warm")
+        nc.scalar.activation(warm[:], ident[:, 0:1], ACT.Exp)
+
+        per_bank = BANK // P
+        cols16 = BANK // 16
+        lists = [offsets[:, h * cols16 : (h + 1) * cols16] for h in range(halves)]
+        score_cols = keep.tile([P, blocks], F32, name="score_cols")
+        for h in range(halves):
+            picked_score = keep.tile([P, BANK], F32, name="picked_score%d" % h)
+            nc.vector.tensor_copy(picked_score[:], score_table[:].indirect(lists[h]))
+            turned = bank(6 + h, "turned%d" % h)
+            for b in range(per_bank):
+                nc.tensor.transpose(turned[:, b * P : (b + 1) * P], picked_score[:, b * P : (b + 1) * P], ident[:])
+            nc.scalar.copy(score_cols[:, h * per_bank : (h + 1) * per_bank], turned[:, SCORE_ROW:BANK:P])
+
+        w1_bf = keep.tile([P, PACK, P, PACK], BF16, name="w1_bf", tag="words0", align_bytes=64)
+        share = P // 4
+        for m0 in range(0, P, share):
+            nc.scalar.copy(
+                w1_bf[:, :, m0 : m0 + share, :].rearrange("p t m j -> p m j t"),
+                w1_raw[:, :, PACK * m0 : PACK * (m0 + share)].rearrange("p j (m t) -> p m j t", t=PACK),
+            )
+
+        picked_scales = keep.tile([P, S], U8, name="picked_scales", tag="score_table", align_bytes=64)
+        nc.vector.tensor_copy(picked_scales[:], scale_table[:].bitcast(U8).indirect(offsets[:]))
+        neg_cols = keep.tile([P, blocks], F32, name="neg_cols", tag="scale_table", align_bytes=64)
+        neg_col_max = keep.tile([P, 1], F32, name="neg_col_max")
+        nc.vector.tensor_scalar(neg_cols[:], score_cols[:], -1.0, None, ALU.mult, ALU.min, accum_out=neg_col_max[:])
+        max_row = bank(3, "max_row")
+        nc.tensor.transpose(max_row[:, 0:P], neg_col_max[:].to_broadcast([P, P]), ident[:])
+        spread = []
+        for h in range(halves):
+            sp = bank(4 + h, "spread%d" % h)
+            for b in range(per_bank):
+                c = h * per_bank + b
+                nc.tensor.transpose(sp[:, b * P : (b + 1) * P], score_cols[:, c : c + 1].to_broadcast([P, P]), ident[:])
+            spread.append(sp)
+
+        w1_codes = keep.tile([P, H], U32, name="w1_codes", align_bytes=64)
+        w1_scales = keep.tile([P, H], U8, name="w1_scales", align_bytes=64)
+        nc.vector.quantize_mx(w1_codes[:].bitcast(FP8X4), w1_scales[:], w1_bf[:].rearrange("p t m j -> p (t m j)"))
+
+        neg_row = keep.tile([P, P], F32, name="neg_row", tag="words0", align_bytes=64)
+        neg_max = keep.tile([P, 1], F32, name="neg_max")
+        nc.vector.tensor_scalar(neg_row[:], max_row[:, 0:P], 1.0, None, ALU.mult, ALU.min, accum_out=neg_max[:])
+        ee = keep.tile([P, S], F32, name="ee")
+        part_total = keep.tile([P, halves], F32, name="part_total")
+        for h in range(halves):
+            nc.scalar.activation(ee[:, h * BANK : (h + 1) * BANK], spread[h][:], ACT.Exp, bias=neg_max[:], accum_out=part_total[:, h : h + 1])
+        total = keep.tile([P, 1], F32, name="total")
+        nc.gpsimd.tensor_tensor(total[:], part_total[:, 0:1], part_total[:, 1:2], ALU.add)
+        minus_one = keep.tile([P, 1], F32, name="minus_one")
+        nc.gpsimd.memset(minus_one[:], -1.0)
+        inv_total = keep.tile([P, 1], F32, name="inv_total")
+        nc.gpsimd.tensor_tensor(inv_total[:], total[:], minus_one[:], ALU.pow)
+
+        picked_words = keep.tile([P, S], U32, name="picked_words", tag="words0", align_bytes=64)
+        for h in range(halves):
+            nc.vector.tensor_copy(picked_words[:, h * BANK : (h + 1) * BANK], word_table[:].indirect(lists[h]))
+
+        w2_raw = keep.tile([P, PACK, N], F32, name="w2_raw", tag="raw")
+        nc.sync.dma_start(w2_raw[:], w2.rearrange("(p j) c -> p j c", j=PACK))
+        w2_bf = keep.tile([P, N, PACK], BF16, name="w2_bf", align_bytes=64)
+        nc.scalar.copy(
+            w2_bf[:].rearrange("p (c i) j -> p c j i", i=4),
+            w2_raw[:].rearrange("p j (c i) -> p c j i", i=4),
+        )
+
+        part_ctx = keep.tile([P, PACK * halves], F32, name="part_ctx")
+        context = keep.tile([P, PACK], F32, name="context")
+        z_planes = [keep.tile([P, PACK, BANK], BF16, name="z_planes%d" % h, align_bytes=64) for h in range(halves)]
+        for t in range(PACK):
+            cols = slice(t * P, (t + 1) * P)
+            y = []
+            for h in range(halves):
+                js = slice(h * BANK, (h + 1) * BANK)
+                u = t * halves + h
+                yb = bank(u, "y%d" % u)
+                nc.tensor.matmul_mx(
+                    yb[:],
+                    lhsT=w1_codes[:, cols].bitcast(FP8X4),
+                    lhsT_scale=w1_scales[:, cols],
+                    rhs=picked_words[:, js].bitcast(FP8X4),
+                    rhs_scale=picked_scales[:, js],
+                    start=True,
+                    stop=True,
+                )
+                weighted = keep.tile([P, BANK], F32, name="weighted%d" % u, tag="weighted%d" % u, align_bytes=64)
+                nc.vector.scalar_tensor_tensor(weighted[:], yb[:], inv_total[:], ee[:, js], ALU.mult, ALU.mult, accum_out=part_ctx[:, u : u + 1])
+                y.append(yb)
+            u = t * halves
+            nc.scalar.activation(context[:, t : t + 1], part_ctx[:, u : u + 1], ACT.Identity, bias=part_ctx[:, u + 1 : u + 2])
+            for h in range(halves):
+                width = BANK if t < PACK - 1 else BANK // 2
+                for c0 in range(0, BANK, width):
+                    nc.scalar.activation(z_planes[h][:, t, c0 : c0 + width], y[h][:, c0 : c0 + width], ACT.Identity, bias=context[:, t : t + 1])
+
+        w2_codes = keep.tile([P, N], U32, name="w2_codes", tag="weighted%d" % (PACK * halves - 1), align_bytes=64)
+        w2_scales = keep.tile([P, N], U8, name="w2_scales", align_bytes=64)
+        nc.vector.quantize_mx(w2_codes[:].bitcast(FP8X4), w2_scales[:], w2_bf[:].rearrange("p c j -> p (c j)"))
+
+        out_rows = out.rearrange("(g p) j -> p g j", p=P)
+        groups = N // P
+        starts = [sum(PIECES[:q]) for q in range(len(PIECES))]
+
+        def interleave(q):
+            j0, width = starts[q], PIECES[q]
+            z_bf = keep.tile([P, width, PACK], BF16, name="z_bf%d" % q, align_bytes=64)
+            c0 = j0 % BANK
+            nc.vector.tensor_copy(
+                z_bf[:].rearrange("p (c i) t -> p c t i", i=4),
+                z_planes[j0 // BANK][:, :, c0 : c0 + width].rearrange("p t (c i) -> p c t i", i=4),
+            )
+            return z_bf
+
+        def finish(q, z_bf):
+            j0, width = starts[q], PIECES[q]
+            z_codes = keep.tile([P, width], U32, name="z_codes%d" % q, align_bytes=64)
+            z_scales = keep.tile([P, width], U8, name="z_scales%d" % q, align_bytes=64)
+            nc.vector.quantize_mx(z_codes[:].bitcast(FP8X4), z_scales[:], z_bf[:].rearrange("p c t -> p (c t)"))
+            acc = bank(q, "acc%d" % q)
+            for g in range(groups):
+                cols = slice(g * P, (g + 1) * P)
+                nc.tensor.matmul_mx(
+                    acc[:, g * width : (g + 1) * width],
+                    lhsT=w2_codes[:, cols].bitcast(FP8X4),
+                    lhsT_scale=w2_scales[:, cols],
+                    rhs=z_codes[:].bitcast(FP8X4),
+                    rhs_scale=z_scales[:],
+                    start=True,
+                    stop=True,
+                )
+            result = keep.tile([P, groups * width], F32, name="result%d" % q)
+            nc.scalar.copy(result[:], acc[:, 0 : groups * width])
+            nc.sync.dma_start(out_rows[:, :, j0 : j0 + width], result[:].rearrange("p (g j) -> p g j", g=groups))
+
+        waiting = None
+        for q in range(len(PIECES)):
+            z_bf = interleave(q)
+            if waiting is not None:
+                finish(q - 1, waiting)
+            waiting = z_bf
+        finish(len(PIECES) - 1, waiting)

@@ -98,12 +98,12 @@ def tile_picked_ygcb_none_p_kernel(tc, x_words, x_scales, w1, w2, score, offs, o
                 nc.tensor.transpose(sp[:, b * P : (b + 1) * P], score_cols[:, c : c + 1].to_broadcast([P, P]), ident[:])
             spread.append(sp)
 
-        w1_codes = keep.tile([P, H], U32, name="w1_codes", align_bytes=64)
+        w1_codes = keep.tile([P, H], U32, name="w1_codes", tag="scale_table", align_bytes=64)
         w1_scales = keep.tile([P, H], U8, name="w1_scales", align_bytes=64)
         nc.vector.quantize_mx(w1_codes[:].bitcast(FP8X4), w1_scales[:], w1_bf[:].rearrange("p t m j -> p (t m j)"))
 
         neg_row = keep.tile([P, P], F32, name="neg_row", tag="words0", align_bytes=64)
-        neg_max = keep.tile([P, 1], F32, name="neg_max")
+        neg_max = keep.tile([P, 1], F32, name="neg_max", tag="w2_bf", align_bytes=64)
         nc.vector.tensor_scalar(neg_row[:], max_row[:, 0:P], 1.0, None, ALU.mult, ALU.min, accum_out=neg_max[:])
         ee = keep.tile([P, S], F32, name="ee")
         part_total = keep.tile([P, halves], F32, name="part_total")
@@ -122,14 +122,13 @@ def tile_picked_ygcb_none_p_kernel(tc, x_words, x_scales, w1, w2, score, offs, o
 
         w2_raw = keep.tile([P, PACK, N], F32, name="w2_raw", tag="raw")
         nc.sync.dma_start(w2_raw[:], w2.rearrange("(p j) c -> p j c", j=PACK))
-        w2_bf = keep.tile([P, N, PACK], BF16, name="w2_bf", align_bytes=64)
+        w2_bf = keep.tile([P, N, PACK], BF16, name="w2_bf", tag="w2_bf", align_bytes=64)
         nc.scalar.copy(
             w2_bf[:].rearrange("p (c i) j -> p c j i", i=4),
             w2_raw[:].rearrange("p j (c i) -> p c j i", i=4),
         )
 
         part_ctx = keep.tile([P, PACK * halves], F32, name="part_ctx")
-        context = keep.tile([P, PACK], F32, name="context")
         z_planes = [keep.tile([P, PACK, BANK], BF16, name="z_planes%d" % h, align_bytes=64) for h in range(halves)]
         for t in range(PACK):
             cols = slice(t * P, (t + 1) * P)
@@ -148,14 +147,16 @@ def tile_picked_ygcb_none_p_kernel(tc, x_words, x_scales, w1, w2, score, offs, o
                     stop=True,
                 )
                 weighted = keep.tile([P, BANK], F32, name="weighted%d" % u, tag="weighted%d" % u, align_bytes=64)
-                nc.vector.scalar_tensor_tensor(weighted[:], yb[:], inv_total[:], ee[:, js], ALU.mult, ALU.mult, accum_out=part_ctx[:, u : u + 1])
+                nc.vector.scalar_tensor_tensor(weighted[:], yb[:], 1.0, ee[:, js], ALU.mult, ALU.mult, accum_out=part_ctx[:, u : u + 1])
                 y.append(yb)
             u = t * halves
-            nc.scalar.activation(context[:, t : t + 1], part_ctx[:, u : u + 1], ACT.Identity, bias=part_ctx[:, u + 1 : u + 2])
+            context = keep.tile([P, 1], F32, name="context%d" % t)
+            engine = nc.gpsimd if t < PACK - 1 else nc.vector
+            engine.tensor_scalar(context[:], part_ctx[:, u : u + 1], part_ctx[:, u + 1 : u + 2], inv_total[:], ALU.add, ALU.mult)
             for h in range(halves):
                 width = BANK if t < PACK - 1 else BANK // 2
                 for c0 in range(0, BANK, width):
-                    nc.scalar.activation(z_planes[h][:, t, c0 : c0 + width], y[h][:, c0 : c0 + width], ACT.Identity, bias=context[:, t : t + 1])
+                    nc.scalar.activation(z_planes[h][:, t, c0 : c0 + width], y[h][:, c0 : c0 + width], ACT.Identity, bias=context[:])
 
         w2_codes = keep.tile([P, N], U32, name="w2_codes", tag="weighted%d" % (PACK * halves - 1), align_bytes=64)
         w2_scales = keep.tile([P, N], U8, name="w2_scales", align_bytes=64)
@@ -193,8 +194,13 @@ def tile_picked_ygcb_none_p_kernel(tc, x_words, x_scales, w1, w2, score, offs, o
                     stop=True,
                 )
             result = keep.tile([P, groups * width], F32, name="result%d" % q)
-            nc.scalar.copy(result[:], acc[:, 0 : groups * width])
-            nc.sync.dma_start(out_rows[:, :, j0 : j0 + width], result[:].rearrange("p (g j) -> p g j", g=groups))
+            last = len(PIECES) - 1
+            if q == last:
+                nc.vector.tensor_copy(result[:], acc[:, 0 : groups * width])
+            else:
+                nc.scalar.copy(result[:], acc[:, 0 : groups * width])
+            queue = nc.scalar if q == last - 1 else nc.sync
+            queue.dma_start(out_rows[:, :, j0 : j0 + width], result[:].rearrange("p (g j) -> p g j", g=groups))
 
         waiting = None
         for q in range(len(PIECES)):

@@ -42,7 +42,7 @@ def tile_picked_ygcb_none_p_kernel(tc, x_words, x_scales, w1, w2, score, offs, o
         nc.sync.dma_start(offsets[:], offs)
         score_table = keep.tile([P, T], F32, name="score_table", tag="score_table", align_bytes=64)
         nc.sync.dma_start(score_table[SCORE_ROW:P, :], score[0:1, :])
-        w1_raw = keep.tile([P, PACK, H], F32, name="w1_raw", tag="raw")
+        w1_raw = keep.tile([P, PACK, H], F32, name="w1_raw")
         nc.sync.dma_start(w1_raw[:], w1.rearrange("(p j) c -> p j c", j=PACK))
         scale_table = keep.tile([P, T // 4], I32, name="scale_table", tag="scale_table", align_bytes=64)
         nc.vector.memset(scale_table[:], 0)
@@ -52,8 +52,7 @@ def tile_picked_ygcb_none_p_kernel(tc, x_words, x_scales, w1, w2, score, offs, o
         nc.gpsimd.memset(zero_s[:], 0.0)
         nc.vector.tensor_copy(score_table[0:SCORE_ROW, 0:ZERO_FIRST], zero[0:SCORE_ROW, :].to_broadcast([SCORE_ROW, ZERO_FIRST]))
         nc.vector.memset(score_table[0:SCORE_ROW, ZERO_FIRST:ZERO_SPLIT], 0.0)
-        for q in range(4):
-            nc.sync.dma_start(scale_table[32 * q : 32 * q + 4, :], x_scales[0, 4 * q : 4 * q + 4, :].bitcast(I32))
+        nc.sync.dma_start(scale_table[0:P:8, :], x_scales[0].bitcast(I32))
         nc.scalar.copy(score_table[0:SCORE_ROW, ZERO_SPLIT:T], zero_s[0:SCORE_ROW, :].to_broadcast([SCORE_ROW, T - ZERO_SPLIT]))
         word_table = keep.tile([P, T], U32, name="word_table", tag="word_table", align_bytes=64)
         nc.sync.dma_start(word_table[:].bitcast(I32), x_words[0].rearrange("p n t -> p (n t)").bitcast(I32))
@@ -66,7 +65,7 @@ def tile_picked_ygcb_none_p_kernel(tc, x_words, x_scales, w1, w2, score, offs, o
         per_bank = BANK // P
         cols16 = BANK // 16
         lists = [offsets[:, h * cols16 : (h + 1) * cols16] for h in range(halves)]
-        score_cols = keep.tile([P, blocks], F32, name="score_cols")
+        score_cols = keep.tile([P, blocks], F32, name="score_cols", tag="w2_raw")
         for h in range(halves):
             picked_score = keep.tile([P, BANK], F32, name="picked_score%d" % h)
             nc.vector.tensor_copy(picked_score[:], score_table[:].indirect(lists[h]))
@@ -83,8 +82,12 @@ def tile_picked_ygcb_none_p_kernel(tc, x_words, x_scales, w1, w2, score, offs, o
                 w1_raw[:, :, PACK * m0 : PACK * (m0 + share)].rearrange("p j (m t) -> p m j t", t=PACK),
             )
 
-        picked_scales = keep.tile([P, S], U8, name="picked_scales", tag="score_table", align_bytes=64)
-        nc.vector.tensor_copy(picked_scales[:], scale_table[:].bitcast(U8).indirect(offsets[:]))
+        apart_scales = keep.tile([P, S], U8, name="apart_scales", tag="score_table", align_bytes=64)
+        nc.vector.tensor_copy(apart_scales[:], scale_table[:].bitcast(U8).indirect(offsets[:]))
+        picked_scales = keep.tile([P, S], U8, name="picked_scales", align_bytes=64)
+        nc.gpsimd.memset(picked_scales[:].bitcast(I32), 0)
+        for q in range(4):
+            nc.sync.dma_start(picked_scales[32 * q : 32 * q + 4, :].bitcast(I32), apart_scales[32 * q : 32 * q + 32 : 8, :].bitcast(I32))
         neg_cols = keep.tile([P, blocks], F32, name="neg_cols", tag="scale_table", align_bytes=64)
         neg_col_max = keep.tile([P, 1], F32, name="neg_col_max")
         nc.vector.tensor_scalar(neg_cols[:], score_cols[:], -1.0, None, ALU.mult, ALU.min, accum_out=neg_col_max[:])
@@ -120,7 +123,7 @@ def tile_picked_ygcb_none_p_kernel(tc, x_words, x_scales, w1, w2, score, offs, o
         for h in range(halves):
             nc.vector.tensor_copy(picked_words[:, h * BANK : (h + 1) * BANK], word_table[:].indirect(lists[h]))
 
-        w2_raw = keep.tile([P, PACK, N], F32, name="w2_raw", tag="raw")
+        w2_raw = keep.tile([P, PACK, N], F32, name="w2_raw", tag="w2_raw")
         nc.sync.dma_start(w2_raw[:], w2.rearrange("(p j) c -> p j c", j=PACK))
         w2_bf = keep.tile([P, N, PACK], BF16, name="w2_bf", tag="w2_bf", align_bytes=64)
         nc.scalar.copy(
@@ -170,7 +173,8 @@ def tile_picked_ygcb_none_p_kernel(tc, x_words, x_scales, w1, w2, score, offs, o
             j0, width = starts[q], PIECES[q]
             z_bf = keep.tile([P, width, PACK], BF16, name="z_bf%d" % q, align_bytes=64)
             c0 = j0 % BANK
-            nc.vector.tensor_copy(
+            weave = nc.vector.tensor_copy if q < len(PIECES) - 2 else nc.scalar.copy
+            weave(
                 z_bf[:].rearrange("p (c i) t -> p c t i", i=4),
                 z_planes[j0 // BANK][:, :, c0 : c0 + width].rearrange("p t (c i) -> p c t i", i=4),
             )
@@ -195,7 +199,7 @@ def tile_picked_ygcb_none_p_kernel(tc, x_words, x_scales, w1, w2, score, offs, o
                 )
             result = keep.tile([P, groups * width], F32, name="result%d" % q)
             last = len(PIECES) - 1
-            if q == last:
+            if q in (last, last - 2):
                 nc.vector.tensor_copy(result[:], acc[:, 0 : groups * width])
             else:
                 nc.scalar.copy(result[:], acc[:, 0 : groups * width])

@@ -19,12 +19,14 @@ U8 = mybir.dt.uint8
 FP8X4 = mybir.dt.float8_e4m3fn_x4
 ALU = mybir.AluOpType
 ACT = mybir.ActivationFunctionType
-AXIS = mybir.AxisListType
 
 SCORE_ROW = P - 1
-ZERO_FIRST = 128
-ZERO_SPLIT = 2560
+SCALE_ROW = P - 16
+ZERO_SPLIT = 2048
 PIECES = (256, 256, 256, 128, 128)
+SCALAR_WEAVES = (3, 4)
+VECTOR_EMPTIES = (2, 4)
+SCALAR_STORES = (3,)
 
 
 def tile_picked_ygcb_none_p_kernel(tc, x_words, x_scales, w1, w2, score, offs, out):
@@ -42,54 +44,52 @@ def tile_picked_ygcb_none_p_kernel(tc, x_words, x_scales, w1, w2, score, offs, o
         nc.sync.dma_start(offsets[:], offs)
         score_table = keep.tile([P, T], F32, name="score_table", tag="score_table", align_bytes=64)
         nc.sync.dma_start(score_table[SCORE_ROW:P, :], score[0:1, :])
-        w1_raw = keep.tile([P, PACK, H], F32, name="w1_raw")
-        nc.sync.dma_start(w1_raw[:], w1.rearrange("(p j) c -> p j c", j=PACK))
         scale_table = keep.tile([P, T // 4], I32, name="scale_table", tag="scale_table", align_bytes=64)
-        nc.vector.memset(scale_table[:], 0)
-        zero = keep.tile([P, 1], F32, name="zero", tag="word_table", align_bytes=64)
-        nc.gpsimd.memset(zero[:], 0.0)
-        zero_s = keep.tile([P, 1], F32, name="zero_s")
-        nc.gpsimd.memset(zero_s[:], 0.0)
-        nc.vector.tensor_copy(score_table[0:SCORE_ROW, 0:ZERO_FIRST], zero[0:SCORE_ROW, :].to_broadcast([SCORE_ROW, ZERO_FIRST]))
-        nc.vector.memset(score_table[0:SCORE_ROW, ZERO_FIRST:ZERO_SPLIT], 0.0)
-        nc.sync.dma_start(scale_table[0:P:8, :], x_scales[0].bitcast(I32))
-        nc.scalar.copy(score_table[0:SCORE_ROW, ZERO_SPLIT:T], zero_s[0:SCORE_ROW, :].to_broadcast([SCORE_ROW, T - ZERO_SPLIT]))
-        word_table = keep.tile([P, T], U32, name="word_table", tag="word_table", align_bytes=64)
+        nc.sync.dma_start(scale_table[SCALE_ROW:P, :], x_scales[0].bitcast(I32))
+        w1_raw = keep.tile([P, PACK, H], F32, name="w1_raw", tag="w1_raw")
+        nc.sync.dma_start(w1_raw[:], w1.rearrange("(p j) c -> p j c", j=PACK))
+        word_table = keep.tile([P, T], U32, name="word_table", align_bytes=64)
         nc.sync.dma_start(word_table[:].bitcast(I32), x_words[0].rearrange("p n t -> p (n t)").bitcast(I32))
+
+        nc.gpsimd.memset(score_table[0:SCORE_ROW, 0:ZERO_SPLIT], 0.0)
+        nc.vector.memset(score_table[0:SCORE_ROW, ZERO_SPLIT : T - 1], 0.0)
+        nc.vector.memset(score_table[0:SCORE_ROW, T - 1 : T], 0.0)
 
         ident = keep.tile([P, P], F32, name="ident")
         make_identity(nc, ident[:])
-        warm = keep.tile([P, 1], F32, name="warm")
-        nc.scalar.activation(warm[:], ident[:, 0:1], ACT.Exp)
+        nc.gpsimd.memset(scale_table[0:SCALE_ROW, :], 0)
+        picked_scales = keep.tile([P, S], U8, name="picked_scales", align_bytes=64)
+        nc.gpsimd.memset(picked_scales[:].bitcast(I32), 0)
+        minus_one = keep.tile([P, 1], F32, name="minus_one")
+        nc.gpsimd.memset(minus_one[:], -1.0)
 
         per_bank = BANK // P
         cols16 = BANK // 16
         lists = [offsets[:, h * cols16 : (h + 1) * cols16] for h in range(halves)]
-        score_cols = keep.tile([P, blocks], F32, name="score_cols", tag="w2_raw")
+        score_cols = keep.tile([P, blocks], F32, name="score_cols")
+        picked_score = keep.tile([P, S], F32, name="picked_score", align_bytes=64)
         for h in range(halves):
-            picked_score = keep.tile([P, BANK], F32, name="picked_score%d" % h)
-            nc.vector.tensor_copy(picked_score[:], score_table[:].indirect(lists[h]))
+            nc.vector.tensor_copy(picked_score[:, h * BANK : (h + 1) * BANK], score_table[:].indirect(lists[h]))
             turned = bank(6 + h, "turned%d" % h)
             for b in range(per_bank):
-                nc.tensor.transpose(turned[:, b * P : (b + 1) * P], picked_score[:, b * P : (b + 1) * P], ident[:])
+                c = h * per_bank + b
+                nc.tensor.transpose(turned[:, b * P : (b + 1) * P], picked_score[:, c * P : (c + 1) * P], ident[:])
             nc.scalar.copy(score_cols[:, h * per_bank : (h + 1) * per_bank], turned[:, SCORE_ROW:BANK:P])
 
-        w1_bf = keep.tile([P, PACK, P, PACK], BF16, name="w1_bf", tag="words0", align_bytes=64)
+        apart_scales = keep.tile([P, S], U8, name="apart_scales", tag="score_table", align_bytes=64)
+        nc.vector.tensor_copy(apart_scales[:], scale_table[:].bitcast(U8).indirect(offsets[:]))
+        for q in range(4):
+            nc.sync.dma_start(picked_scales[32 * q : 32 * q + 4, :].bitcast(I32), apart_scales[SCALE_ROW + 4 * q : SCALE_ROW + 4 * q + 4, :].bitcast(I32))
+
+        w1_bf = keep.tile([P, PACK, P, PACK], BF16, name="w1_bf", tag="words", align_bytes=64)
         share = P // 4
         for m0 in range(0, P, share):
             nc.scalar.copy(
                 w1_bf[:, :, m0 : m0 + share, :].rearrange("p t m j -> p m j t"),
                 w1_raw[:, :, PACK * m0 : PACK * (m0 + share)].rearrange("p j (m t) -> p m j t", t=PACK),
             )
-
-        apart_scales = keep.tile([P, S], U8, name="apart_scales", tag="score_table", align_bytes=64)
-        nc.vector.tensor_copy(apart_scales[:], scale_table[:].bitcast(U8).indirect(offsets[:]))
-        picked_scales = keep.tile([P, S], U8, name="picked_scales", align_bytes=64)
-        nc.gpsimd.memset(picked_scales[:].bitcast(I32), 0)
-        for q in range(4):
-            nc.sync.dma_start(picked_scales[32 * q : 32 * q + 4, :].bitcast(I32), apart_scales[32 * q : 32 * q + 32 : 8, :].bitcast(I32))
         neg_cols = keep.tile([P, blocks], F32, name="neg_cols", tag="scale_table", align_bytes=64)
-        neg_col_max = keep.tile([P, 1], F32, name="neg_col_max")
+        neg_col_max = keep.tile([P, 1], F32, name="neg_col_max", tag="w2_raw")
         nc.vector.tensor_scalar(neg_cols[:], score_cols[:], -1.0, None, ALU.mult, ALU.min, accum_out=neg_col_max[:])
         max_row = bank(3, "max_row")
         nc.tensor.transpose(max_row[:, 0:P], neg_col_max[:].to_broadcast([P, P]), ident[:])
@@ -105,23 +105,21 @@ def tile_picked_ygcb_none_p_kernel(tc, x_words, x_scales, w1, w2, score, offs, o
         w1_scales = keep.tile([P, H], U8, name="w1_scales", align_bytes=64)
         nc.vector.quantize_mx(w1_codes[:].bitcast(FP8X4), w1_scales[:], w1_bf[:].rearrange("p t m j -> p (t m j)"))
 
-        neg_row = keep.tile([P, P], F32, name="neg_row", tag="words0", align_bytes=64)
+        neg_row = keep.tile([P, P], F32, name="neg_row", tag="words", align_bytes=64)
         neg_max = keep.tile([P, 1], F32, name="neg_max", tag="w2_bf", align_bytes=64)
         nc.vector.tensor_scalar(neg_row[:], max_row[:, 0:P], 1.0, None, ALU.mult, ALU.min, accum_out=neg_max[:])
+        words = keep.tile([P, S], U32, name="words", tag="words", align_bytes=64)
+        for h in range(halves):
+            nc.vector.tensor_copy(words[:, h * BANK : (h + 1) * BANK], word_table[:].indirect(lists[h]))
+
         ee = keep.tile([P, S], F32, name="ee")
         part_total = keep.tile([P, halves], F32, name="part_total")
         for h in range(halves):
             nc.scalar.activation(ee[:, h * BANK : (h + 1) * BANK], spread[h][:], ACT.Exp, bias=neg_max[:], accum_out=part_total[:, h : h + 1])
         total = keep.tile([P, 1], F32, name="total")
         nc.gpsimd.tensor_tensor(total[:], part_total[:, 0:1], part_total[:, 1:2], ALU.add)
-        minus_one = keep.tile([P, 1], F32, name="minus_one")
-        nc.gpsimd.memset(minus_one[:], -1.0)
         inv_total = keep.tile([P, 1], F32, name="inv_total")
         nc.gpsimd.tensor_tensor(inv_total[:], total[:], minus_one[:], ALU.pow)
-
-        picked_words = keep.tile([P, S], U32, name="picked_words", tag="words0", align_bytes=64)
-        for h in range(halves):
-            nc.vector.tensor_copy(picked_words[:, h * BANK : (h + 1) * BANK], word_table[:].indirect(lists[h]))
 
         w2_raw = keep.tile([P, PACK, N], F32, name="w2_raw", tag="w2_raw")
         nc.sync.dma_start(w2_raw[:], w2.rearrange("(p j) c -> p j c", j=PACK))
@@ -131,8 +129,9 @@ def tile_picked_ygcb_none_p_kernel(tc, x_words, x_scales, w1, w2, score, offs, o
             w2_raw[:].rearrange("p j (c i) -> p c j i", i=4),
         )
 
+        starts = [sum(PIECES[:q]) for q in range(len(PIECES))]
         part_ctx = keep.tile([P, PACK * halves], F32, name="part_ctx")
-        z_planes = [keep.tile([P, PACK, BANK], BF16, name="z_planes%d" % h, align_bytes=64) for h in range(halves)]
+        z_planes = keep.tile([P, PACK, S], BF16, name="z_planes", align_bytes=64)
         for t in range(PACK):
             cols = slice(t * P, (t + 1) * P)
             y = []
@@ -144,7 +143,7 @@ def tile_picked_ygcb_none_p_kernel(tc, x_words, x_scales, w1, w2, score, offs, o
                     yb[:],
                     lhsT=w1_codes[:, cols].bitcast(FP8X4),
                     lhsT_scale=w1_scales[:, cols],
-                    rhs=picked_words[:, js].bitcast(FP8X4),
+                    rhs=words[:, js].bitcast(FP8X4),
                     rhs_scale=picked_scales[:, js],
                     start=True,
                     stop=True,
@@ -156,10 +155,10 @@ def tile_picked_ygcb_none_p_kernel(tc, x_words, x_scales, w1, w2, score, offs, o
             context = keep.tile([P, 1], F32, name="context%d" % t)
             engine = nc.gpsimd if t < PACK - 1 else nc.vector
             engine.tensor_scalar(context[:], part_ctx[:, u : u + 1], part_ctx[:, u + 1 : u + 2], inv_total[:], ALU.add, ALU.mult)
-            for h in range(halves):
-                width = BANK if t < PACK - 1 else BANK // 2
-                for c0 in range(0, BANK, width):
-                    nc.scalar.activation(z_planes[h][:, t, c0 : c0 + width], y[h][:, c0 : c0 + width], ACT.Identity, bias=context[:])
+            cuts = [0, BANK, S] if t < PACK - 1 else sorted(set(starts + [BANK, S]))
+            for c0, c1 in zip(cuts, cuts[1:]):
+                h = c0 // BANK
+                nc.scalar.activation(z_planes[:, t, c0:c1], y[h][:, c0 - h * BANK : c1 - h * BANK], ACT.Identity, bias=context[:])
 
         w2_codes = keep.tile([P, N], U32, name="w2_codes", tag="weighted%d" % (PACK * halves - 1), align_bytes=64)
         w2_scales = keep.tile([P, N], U8, name="w2_scales", align_bytes=64)
@@ -167,16 +166,14 @@ def tile_picked_ygcb_none_p_kernel(tc, x_words, x_scales, w1, w2, score, offs, o
 
         out_rows = out.rearrange("(g p) j -> p g j", p=P)
         groups = N // P
-        starts = [sum(PIECES[:q]) for q in range(len(PIECES))]
 
         def interleave(q):
             j0, width = starts[q], PIECES[q]
             z_bf = keep.tile([P, width, PACK], BF16, name="z_bf%d" % q, align_bytes=64)
-            c0 = j0 % BANK
-            weave = nc.vector.tensor_copy if q < len(PIECES) - 2 else nc.scalar.copy
+            weave = nc.scalar.copy if q in SCALAR_WEAVES else nc.vector.tensor_copy
             weave(
                 z_bf[:].rearrange("p (c i) t -> p c t i", i=4),
-                z_planes[j0 // BANK][:, :, c0 : c0 + width].rearrange("p t (c i) -> p c t i", i=4),
+                z_planes[:, :, j0 : j0 + width].rearrange("p t (c i) -> p c t i", i=4),
             )
             return z_bf
 
@@ -198,12 +195,9 @@ def tile_picked_ygcb_none_p_kernel(tc, x_words, x_scales, w1, w2, score, offs, o
                     stop=True,
                 )
             result = keep.tile([P, groups * width], F32, name="result%d" % q)
-            last = len(PIECES) - 1
-            if q in (last, last - 2):
-                nc.vector.tensor_copy(result[:], acc[:, 0 : groups * width])
-            else:
-                nc.scalar.copy(result[:], acc[:, 0 : groups * width])
-            queue = nc.scalar if q == last - 1 else nc.sync
+            empty = nc.vector.tensor_copy if q in VECTOR_EMPTIES else nc.scalar.copy
+            empty(result[:], acc[:, 0 : groups * width])
+            queue = nc.scalar if q in SCALAR_STORES else nc.sync
             queue.dma_start(out_rows[:, :, j0 : j0 + width], result[:].rearrange("p (g j) -> p g j", g=groups))
 
         waiting = None

@@ -66,17 +66,16 @@ def tile_picked_ygcb_none_p_kernel(tc, x_words, x_scales, w1, w2, score, offs, o
         per_bank = BANK // P
         cols16 = BANK // 16
         lists = [offsets[:, h * cols16 : (h + 1) * cols16] for h in range(halves)]
-        score_cols = keep.tile([P, blocks], F32, name="score_cols")
+        turned = []
         picked_score = keep.tile([P, S], F32, name="picked_score", align_bytes=64)
         for h in range(halves):
             nc.vector.tensor_copy(picked_score[:, h * BANK : (h + 1) * BANK], score_table[:].indirect(lists[h]))
-            turned = bank(6 + h, "turned%d" % h)
+            turned.append(bank(6 + h, "turned%d" % h))
             for b in range(per_bank):
                 c = h * per_bank + b
-                nc.tensor.transpose(turned[:, b * P : (b + 1) * P], picked_score[:, c * P : (c + 1) * P], ident[:])
-            nc.scalar.copy(score_cols[:, h * per_bank : (h + 1) * per_bank], turned[:, SCORE_ROW:BANK:P])
+                nc.tensor.transpose(turned[h][:, b * P : (b + 1) * P], picked_score[:, c * P : (c + 1) * P], ident[:])
 
-        apart_scales = keep.tile([P, S], U8, name="apart_scales", tag="score_table", align_bytes=64)
+        apart_scales = keep.tile([P, S], U8, name="apart_scales", align_bytes=64)
         nc.vector.tensor_copy(apart_scales[:], scale_table[:].bitcast(U8).indirect(offsets[:]))
         for q in range(4):
             nc.sync.dma_start(picked_scales[32 * q : 32 * q + 4, :].bitcast(I32), apart_scales[SCALE_ROW + 4 * q : SCALE_ROW + 4 * q + 4, :].bitcast(I32))
@@ -88,9 +87,11 @@ def tile_picked_ygcb_none_p_kernel(tc, x_words, x_scales, w1, w2, score, offs, o
                 w1_bf[:, :, m0 : m0 + share, :].rearrange("p t m j -> p m j t"),
                 w1_raw[:, :, PACK * m0 : PACK * (m0 + share)].rearrange("p j (m t) -> p m j t", t=PACK),
             )
-        neg_cols = keep.tile([P, blocks], F32, name="neg_cols", tag="scale_table", align_bytes=64)
+        neg_cols = keep.tile([P, blocks], F32, name="neg_cols")
+        neg_first = keep.tile([P, 1], F32, name="neg_first")
         neg_col_max = keep.tile([P, 1], F32, name="neg_col_max", tag="w2_raw")
-        nc.vector.tensor_scalar(neg_cols[:], score_cols[:], -1.0, None, ALU.mult, ALU.min, accum_out=neg_col_max[:])
+        nc.vector.tensor_scalar(neg_cols[:, 0:per_bank], turned[0][:, SCORE_ROW:BANK:P], -1.0, None, ALU.mult, ALU.min, accum_out=neg_first[:])
+        nc.vector.tensor_scalar(neg_cols[:, per_bank:blocks], turned[1][:, SCORE_ROW:BANK:P], -1.0, neg_first[:], ALU.mult, ALU.min, accum_out=neg_col_max[:])
         max_row = bank(3, "max_row")
         nc.tensor.transpose(max_row[:, 0:P], neg_col_max[:].to_broadcast([P, P]), ident[:])
         spread = []
@@ -98,24 +99,24 @@ def tile_picked_ygcb_none_p_kernel(tc, x_words, x_scales, w1, w2, score, offs, o
             sp = bank(4 + h, "spread%d" % h)
             for b in range(per_bank):
                 c = h * per_bank + b
-                nc.tensor.transpose(sp[:, b * P : (b + 1) * P], score_cols[:, c : c + 1].to_broadcast([P, P]), ident[:])
+                nc.tensor.transpose(sp[:, b * P : (b + 1) * P], neg_cols[:, c : c + 1].to_broadcast([P, P]), ident[:])
             spread.append(sp)
 
-        w1_codes = keep.tile([P, H], U32, name="w1_codes", tag="scale_table", align_bytes=64)
+        w1_codes = keep.tile([P, H], U32, name="w1_codes", align_bytes=64)
         w1_scales = keep.tile([P, H], U8, name="w1_scales", align_bytes=64)
         nc.vector.quantize_mx(w1_codes[:].bitcast(FP8X4), w1_scales[:], w1_bf[:].rearrange("p t m j -> p (t m j)"))
 
         neg_row = keep.tile([P, P], F32, name="neg_row", tag="words", align_bytes=64)
         neg_max = keep.tile([P, 1], F32, name="neg_max", tag="w2_bf", align_bytes=64)
         nc.vector.tensor_scalar(neg_row[:], max_row[:, 0:P], 1.0, None, ALU.mult, ALU.min, accum_out=neg_max[:])
-        words = keep.tile([P, S], U32, name="words", tag="words", align_bytes=64)
+        words = keep.tile([P, S], U32, name="words", align_bytes=64)
         for h in range(halves):
             nc.vector.tensor_copy(words[:, h * BANK : (h + 1) * BANK], word_table[:].indirect(lists[h]))
 
         ee = keep.tile([P, S], F32, name="ee")
         part_total = keep.tile([P, halves], F32, name="part_total")
         for h in range(halves):
-            nc.scalar.activation(ee[:, h * BANK : (h + 1) * BANK], spread[h][:], ACT.Exp, bias=neg_max[:], accum_out=part_total[:, h : h + 1])
+            nc.scalar.activation(ee[:, h * BANK : (h + 1) * BANK], spread[h][:], ACT.Exp, bias=neg_max[:], scale=-1.0, accum_out=part_total[:, h : h + 1])
         total = keep.tile([P, 1], F32, name="total")
         nc.gpsimd.tensor_tensor(total[:], part_total[:, 0:1], part_total[:, 1:2], ALU.add)
         inv_total = keep.tile([P, 1], F32, name="inv_total")
@@ -149,13 +150,19 @@ def tile_picked_ygcb_none_p_kernel(tc, x_words, x_scales, w1, w2, score, offs, o
                     stop=True,
                 )
                 weighted = keep.tile([P, BANK], F32, name="weighted%d" % u, tag="weighted%d" % u, align_bytes=64)
-                nc.vector.scalar_tensor_tensor(weighted[:], yb[:], 1.0, ee[:, js], ALU.mult, ALU.mult, accum_out=part_ctx[:, u : u + 1])
+                factor = 1.0 if t < PACK - 1 else inv_total[:]
+                nc.vector.scalar_tensor_tensor(weighted[:], yb[:], factor, ee[:, js], ALU.mult, ALU.mult, accum_out=part_ctx[:, u : u + 1])
                 y.append(yb)
             u = t * halves
             context = keep.tile([P, 1], F32, name="context%d" % t)
-            engine = nc.gpsimd if t < PACK - 1 else nc.vector
-            engine.tensor_scalar(context[:], part_ctx[:, u : u + 1], part_ctx[:, u + 1 : u + 2], inv_total[:], ALU.add, ALU.mult)
-            cuts = [0, BANK, S] if t < PACK - 1 else sorted(set(starts + [BANK, S]))
+            first, second = part_ctx[:, u : u + 1], part_ctx[:, u + 1 : u + 2]
+            if t < PACK - 1:
+                nc.gpsimd.tensor_scalar(context[:], first, second, inv_total[:], ALU.add, ALU.mult)
+                cuts = [0, BANK, S]
+            else:
+                nc.gpsimd.tensor_tensor(context[:], first, second, ALU.add)
+                nc.vector.tensor_scalar(z_planes[:, t, 0 : PIECES[0]], y[0][:, 0 : PIECES[0]], first, second, ALU.add, ALU.add)
+                cuts = sorted(set(starts[1:] + [BANK, S]))
             for c0, c1 in zip(cuts, cuts[1:]):
                 h = c0 // BANK
                 nc.scalar.activation(z_planes[:, t, c0:c1], y[h][:, c0 - h * BANK : c1 - h * BANK], ACT.Identity, bias=context[:])

@@ -25,8 +25,7 @@ SCALE_ROW = P - 16
 ZERO_SPLIT = 2048
 PIECES = (256, 256, 256, 128, 128)
 SCALAR_WEAVES = (3, 4)
-VECTOR_EMPTIES = (2, 4)
-SCALAR_STORES = (3,)
+LAST_BANK = 5
 
 
 def tile_picked_ygcb_none_p_kernel(tc, x_words, x_scales, w1, w2, score, offs, out):
@@ -88,12 +87,13 @@ def tile_picked_ygcb_none_p_kernel(tc, x_words, x_scales, w1, w2, score, offs, o
                 w1_raw[:, :, PACK * m0 : PACK * (m0 + share)].rearrange("p j (m t) -> p m j t", t=PACK),
             )
         neg_cols = keep.tile([P, blocks], F32, name="neg_cols")
-        neg_first = keep.tile([P, 1], F32, name="neg_first")
-        neg_col_max = keep.tile([P, 1], F32, name="neg_col_max", tag="w2_raw")
-        nc.vector.tensor_scalar(neg_cols[:, 0:per_bank], turned[0][:, SCORE_ROW:BANK:P], -1.0, None, ALU.mult, ALU.min, accum_out=neg_first[:])
-        nc.vector.tensor_scalar(neg_cols[:, per_bank:blocks], turned[1][:, SCORE_ROW:BANK:P], -1.0, neg_first[:], ALU.mult, ALU.min, accum_out=neg_col_max[:])
+        neg_col_max = keep.tile([P, halves], F32, name="neg_col_max", tag="w2_raw")
         max_row = bank(3, "max_row")
-        nc.tensor.transpose(max_row[:, 0:P], neg_col_max[:].to_broadcast([P, P]), ident[:])
+        for h in range(halves):
+            nc.vector.tensor_scalar(
+                neg_cols[:, h * per_bank : (h + 1) * per_bank], turned[h][:, SCORE_ROW:BANK:P], -1.0, None, ALU.mult, ALU.min, accum_out=neg_col_max[:, h : h + 1]
+            )
+            nc.tensor.transpose(max_row[:, h * P : (h + 1) * P], neg_col_max[:, h : h + 1].to_broadcast([P, P]), ident[:])
         spread = []
         for h in range(halves):
             sp = bank(4 + h, "spread%d" % h)
@@ -106,9 +106,9 @@ def tile_picked_ygcb_none_p_kernel(tc, x_words, x_scales, w1, w2, score, offs, o
         w1_scales = keep.tile([P, H], U8, name="w1_scales", align_bytes=64)
         nc.vector.quantize_mx(w1_codes[:].bitcast(FP8X4), w1_scales[:], w1_bf[:].rearrange("p t m j -> p (t m j)"))
 
-        neg_row = keep.tile([P, P], F32, name="neg_row", tag="words", align_bytes=64)
+        neg_row = keep.tile([P, halves * P], F32, name="neg_row", tag="words", align_bytes=64)
         neg_max = keep.tile([P, 1], F32, name="neg_max", tag="w2_bf", align_bytes=64)
-        nc.vector.tensor_scalar(neg_row[:], max_row[:, 0:P], 1.0, None, ALU.mult, ALU.min, accum_out=neg_max[:])
+        nc.vector.tensor_scalar(neg_row[:], max_row[:, 0 : halves * P], 1.0, None, ALU.mult, ALU.min, accum_out=neg_max[:])
         words = keep.tile([P, S], U32, name="words", align_bytes=64)
         for h in range(halves):
             nc.vector.tensor_copy(words[:, h * BANK : (h + 1) * BANK], word_table[:].indirect(lists[h]))
@@ -162,55 +162,89 @@ def tile_picked_ygcb_none_p_kernel(tc, x_words, x_scales, w1, w2, score, offs, o
             else:
                 nc.gpsimd.tensor_tensor(context[:], first, second, ALU.add)
                 nc.vector.tensor_scalar(z_planes[:, t, 0 : PIECES[0]], y[0][:, 0 : PIECES[0]], first, second, ALU.add, ALU.add)
-                cuts = sorted(set(starts[1:] + [BANK, S]))
+                cuts = [PIECES[0], BANK, BANK + PIECES[2], S]
             for c0, c1 in zip(cuts, cuts[1:]):
                 h = c0 // BANK
                 nc.scalar.activation(z_planes[:, t, c0:c1], y[h][:, c0 - h * BANK : c1 - h * BANK], ACT.Identity, bias=context[:])
+
+        for b in (5, 6, 7,):
+            idle = bank(b, "idle%d" % b)
+            nc.tensor.matmul_mx(
+                idle[:],
+                lhsT=w1_codes[:, 0:P].bitcast(FP8X4),
+                lhsT_scale=w1_scales[:, 0:P],
+                rhs=words[:, 0:BANK].bitcast(FP8X4),
+                rhs_scale=picked_scales[:, 0:BANK],
+                start=True,
+                stop=True,
+            )
 
         w2_codes = keep.tile([P, N], U32, name="w2_codes", tag="weighted%d" % (PACK * halves - 1), align_bytes=64)
         w2_scales = keep.tile([P, N], U8, name="w2_scales", align_bytes=64)
         nc.vector.quantize_mx(w2_codes[:].bitcast(FP8X4), w2_scales[:], w2_bf[:].rearrange("p c j -> p (c j)"))
 
-        out_rows = out.rearrange("(g p) j -> p g j", p=P)
         groups = N // P
 
-        def interleave(q):
+        def weave(q):
             j0, width = starts[q], PIECES[q]
             z_bf = keep.tile([P, width, PACK], BF16, name="z_bf%d" % q, align_bytes=64)
-            weave = nc.scalar.copy if q in SCALAR_WEAVES else nc.vector.tensor_copy
-            weave(
+            copy = nc.scalar.copy if q in SCALAR_WEAVES else nc.vector.tensor_copy
+            copy(
                 z_bf[:].rearrange("p (c i) t -> p c t i", i=4),
                 z_planes[:, :, j0 : j0 + width].rearrange("p t (c i) -> p c t i", i=4),
             )
             return z_bf
 
-        def finish(q, z_bf):
-            j0, width = starts[q], PIECES[q]
+        def quantise(q, z_bf):
+            width = PIECES[q]
             z_codes = keep.tile([P, width], U32, name="z_codes%d" % q, align_bytes=64)
             z_scales = keep.tile([P, width], U8, name="z_scales%d" % q, align_bytes=64)
             nc.vector.quantize_mx(z_codes[:].bitcast(FP8X4), z_scales[:], z_bf[:].rearrange("p c t -> p (c t)"))
+            return z_codes, z_scales
+
+        def product(acc, g, z_codes, z_scales):
+            cols = slice(g * P, (g + 1) * P)
+            nc.tensor.matmul_mx(
+                acc,
+                lhsT=w2_codes[:, cols].bitcast(FP8X4),
+                lhsT_scale=w2_scales[:, cols],
+                rhs=z_codes[:].bitcast(FP8X4),
+                rhs_scale=z_scales[:],
+                start=True,
+                stop=True,
+            )
+
+        def finish(q, z_bf):
+            j0, width = starts[q], PIECES[q]
+            z_codes, z_scales = quantise(q, z_bf)
             acc = bank(q, "acc%d" % q)
             for g in range(groups):
-                cols = slice(g * P, (g + 1) * P)
-                nc.tensor.matmul_mx(
-                    acc[:, g * width : (g + 1) * width],
-                    lhsT=w2_codes[:, cols].bitcast(FP8X4),
-                    lhsT_scale=w2_scales[:, cols],
-                    rhs=z_codes[:].bitcast(FP8X4),
-                    rhs_scale=z_scales[:],
-                    start=True,
-                    stop=True,
-                )
+                product(acc[:, g * width : (g + 1) * width], g, z_codes, z_scales)
+            if q == 0:
+                for g in range(groups):
+                    result = keep.tile([P, width], F32, name="result_first%d" % g)
+                    nc.scalar.copy(result[:], acc[:, g * width : (g + 1) * width])
+                    nc.sync.dma_start(out[g * P : (g + 1) * P, j0 : j0 + width], result[:])
+                return
             result = keep.tile([P, groups * width], F32, name="result%d" % q)
-            empty = nc.vector.tensor_copy if q in VECTOR_EMPTIES else nc.scalar.copy
-            empty(result[:], acc[:, 0 : groups * width])
-            queue = nc.scalar if q in SCALAR_STORES else nc.sync
-            queue.dma_start(out_rows[:, :, j0 : j0 + width], result[:].rearrange("p (g j) -> p g j", g=groups))
+            nc.scalar.copy(result[:], acc[:, 0 : groups * width])
+            rows = out.rearrange("(g p) j -> p g j", p=P)
+            nc.sync.dma_start(rows[:, :, j0 : j0 + width], result[:].rearrange("p (g j) -> p g j", g=groups))
 
-        waiting = None
-        for q in range(len(PIECES)):
-            z_bf = interleave(q)
-            if waiting is not None:
-                finish(q - 1, waiting)
-            waiting = z_bf
-        finish(len(PIECES) - 1, waiting)
+        def finish_shared(q, z_bf):
+            j0, width = starts[q], PIECES[q]
+            z_codes, z_scales = quantise(q, z_bf)
+            for g, (b, empty, queue) in enumerate(((q, nc.vector.tensor_copy, nc.sync), (LAST_BANK, nc.scalar.copy, nc.scalar))):
+                acc = bank(b, "acc_last%d" % g)
+                product(acc[:, 0:width], g, z_codes, z_scales)
+                result = keep.tile([P, width], F32, name="result_last%d" % g)
+                empty(result[:], acc[:, 0:width])
+                queue.dma_start(out[g * P : (g + 1) * P, j0 : j0 + width], result[:])
+
+        woven = [weave(0), weave(1), None, weave(3), weave(4)]
+        finish(0, woven[0])
+        finish(1, woven[1])
+        woven[2] = weave(2)
+        finish(3, woven[3])
+        finish(4, woven[4])
+        finish_shared(2, woven[2])

@@ -24,7 +24,7 @@ SCORE_ROW = P - 1
 SCALE_ROW = P - 16
 ZERO_SPLIT = 2048
 PIECES = (256, 256, 256, 128, 128)
-SCALAR_WEAVES = (3, 4)
+SCALAR_WEAVES = (0, 0, 64, 128, 128)
 LAST_BANK = 5
 
 
@@ -179,20 +179,26 @@ def tile_picked_ygcb_none_p_kernel(tc, x_words, x_scales, w1, w2, score, offs, o
                 stop=True,
             )
 
-        w2_codes = keep.tile([P, N], U32, name="w2_codes", tag="weighted%d" % (PACK * halves - 1), align_bytes=64)
-        w2_scales = keep.tile([P, N], U8, name="w2_scales", align_bytes=64)
-        nc.vector.quantize_mx(w2_codes[:].bitcast(FP8X4), w2_scales[:], w2_bf[:].rearrange("p c j -> p (c j)"))
+        w2_codes, w2_scales = [], []
+        for g in range(N // P):
+            codes = keep.tile([P, P], U32, name="w2_codes%d" % g, tag="weighted%d" % (PACK * halves - 2 + g), align_bytes=64)
+            scales = keep.tile([P, P], U8, name="w2_scales%d" % g, align_bytes=64)
+            nc.vector.quantize_mx(codes[:].bitcast(FP8X4), scales[:], w2_bf[:, g * P : (g + 1) * P, :].rearrange("p c j -> p (c j)"))
+            w2_codes.append(codes)
+            w2_scales.append(scales)
 
         groups = N // P
 
         def weave(q):
             j0, width = starts[q], PIECES[q]
             z_bf = keep.tile([P, width, PACK], BF16, name="z_bf%d" % q, align_bytes=64)
-            copy = nc.scalar.copy if q in SCALAR_WEAVES else nc.vector.tensor_copy
-            copy(
-                z_bf[:].rearrange("p (c i) t -> p c t i", i=4),
-                z_planes[:, :, j0 : j0 + width].rearrange("p t (c i) -> p c t i", i=4),
-            )
+            cut = width - SCALAR_WEAVES[q]
+            for copy, c0, c1 in ((nc.vector.tensor_copy, 0, cut), (nc.scalar.copy, cut, width)):
+                if c1 > c0:
+                    copy(
+                        z_bf[:, c0:c1, :].rearrange("p (c i) t -> p c t i", i=4),
+                        z_planes[:, :, j0 + c0 : j0 + c1].rearrange("p t (c i) -> p c t i", i=4),
+                    )
             return z_bf
 
         def quantise(q, z_bf):
@@ -203,11 +209,10 @@ def tile_picked_ygcb_none_p_kernel(tc, x_words, x_scales, w1, w2, score, offs, o
             return z_codes, z_scales
 
         def product(acc, g, z_codes, z_scales):
-            cols = slice(g * P, (g + 1) * P)
             nc.tensor.matmul_mx(
                 acc,
-                lhsT=w2_codes[:, cols].bitcast(FP8X4),
-                lhsT_scale=w2_scales[:, cols],
+                lhsT=w2_codes[g][:].bitcast(FP8X4),
+                lhsT_scale=w2_scales[g][:],
                 rhs=z_codes[:].bitcast(FP8X4),
                 rhs_scale=z_scales[:],
                 start=True,

@@ -65,51 +65,52 @@ def tile_picked_ygcb_none_p_kernel(tc, x_words, x_scales, w1, w2, score, offs, o
         per_bank = BANK // P
         cols16 = BANK // 16
         lists = [offsets[:, h * cols16 : (h + 1) * cols16] for h in range(halves)]
-        turned = []
+        turned = bank(6, "turned")
         picked_score = keep.tile([P, S], F32, name="picked_score", align_bytes=64)
         for h in range(halves):
             nc.vector.tensor_copy(picked_score[:, h * BANK : (h + 1) * BANK], score_table[:].indirect(lists[h]))
-            turned.append(bank(6 + h, "turned%d" % h))
             for b in range(per_bank):
                 c = h * per_bank + b
-                nc.tensor.transpose(turned[h][:, b * P : (b + 1) * P], picked_score[:, c * P : (c + 1) * P], ident[:])
+                left = 2 * (blocks - 1 - c)
+                nc.tensor.transpose(turned[:, left : left + P], picked_score[:, c * P : (c + 1) * P], ident[:])
 
         apart_scales = keep.tile([P, S], U8, name="apart_scales", align_bytes=64)
         nc.vector.tensor_copy(apart_scales[:], scale_table[:].bitcast(U8).indirect(offsets[:]))
         for q in range(4):
             nc.sync.dma_start(picked_scales[32 * q : 32 * q + 4, :].bitcast(I32), apart_scales[SCALE_ROW + 4 * q : SCALE_ROW + 4 * q + 4, :].bitcast(I32))
 
-        w1_bf = keep.tile([P, PACK, P, PACK], BF16, name="w1_bf", tag="words", align_bytes=64)
-        share = P // 4
-        for m0 in range(0, P, share):
-            nc.scalar.copy(
-                w1_bf[:, :, m0 : m0 + share, :].rearrange("p t m j -> p m j t"),
-                w1_raw[:, :, PACK * m0 : PACK * (m0 + share)].rearrange("p j (m t) -> p m j t", t=PACK),
-            )
+        pairs = PACK // 2
+        share = P // 2
+        w1_bf = []
+        for g in range(pairs):
+            cast = keep.tile([P, 2, P, PACK], BF16, name="w1_bf%d" % g, align_bytes=64)
+            columns = w1_raw[:].rearrange("p j (m t) -> p m j t", t=PACK)
+            for m0 in range(0, P, share):
+                nc.scalar.copy(cast[:, :, m0 : m0 + share, :].rearrange("p t m j -> p m j t"), columns[:, m0 : m0 + share, :, 2 * g : 2 * g + 2])
+            w1_bf.append(cast)
         neg_cols = keep.tile([P, blocks], F32, name="neg_cols")
-        neg_col_max = keep.tile([P, halves], F32, name="neg_col_max", tag="w2_raw")
+        neg_col_max = keep.tile([P, 1], F32, name="neg_col_max", tag="w2_raw")
         max_row = bank(3, "max_row")
-        for h in range(halves):
-            nc.vector.tensor_scalar(
-                neg_cols[:, h * per_bank : (h + 1) * per_bank], turned[h][:, SCORE_ROW:BANK:P], -1.0, None, ALU.mult, ALU.min, accum_out=neg_col_max[:, h : h + 1]
-            )
-            nc.tensor.transpose(max_row[:, h * P : (h + 1) * P], neg_col_max[:, h : h + 1].to_broadcast([P, P]), ident[:])
+        nc.vector.tensor_scalar(neg_cols[:], turned[:, SCORE_ROW : SCORE_ROW + 2 * blocks : 2], -1.0, None, ALU.mult, ALU.min, accum_out=neg_col_max[:])
+        nc.tensor.transpose(max_row[:, 0:P], neg_col_max[:].to_broadcast([P, P]), ident[:])
         spread = []
         for h in range(halves):
             sp = bank(4 + h, "spread%d" % h)
             for b in range(per_bank):
-                c = h * per_bank + b
+                c = blocks - 1 - (h * per_bank + b)
                 nc.tensor.transpose(sp[:, b * P : (b + 1) * P], neg_cols[:, c : c + 1].to_broadcast([P, P]), ident[:])
             spread.append(sp)
 
         w1_codes = keep.tile([P, H], U32, name="w1_codes", align_bytes=64)
         w1_scales = keep.tile([P, H], U8, name="w1_scales", align_bytes=64)
-        nc.vector.quantize_mx(w1_codes[:].bitcast(FP8X4), w1_scales[:], w1_bf[:].rearrange("p t m j -> p (t m j)"))
+        for g in range(pairs):
+            cols = slice(2 * g * P, 2 * (g + 1) * P)
+            nc.vector.quantize_mx(w1_codes[:, cols].bitcast(FP8X4), w1_scales[:, cols], w1_bf[g][:].rearrange("p t m j -> p (t m j)"))
 
-        neg_row = keep.tile([P, halves * P], F32, name="neg_row", tag="words", align_bytes=64)
+        neg_row = keep.tile([P, P], F32, name="neg_row", tag="w1_bf0", align_bytes=64)
         neg_max = keep.tile([P, 1], F32, name="neg_max", tag="w2_bf", align_bytes=64)
-        nc.vector.tensor_scalar(neg_row[:], max_row[:, 0 : halves * P], 1.0, None, ALU.mult, ALU.min, accum_out=neg_max[:])
-        words = keep.tile([P, S], U32, name="words", align_bytes=64)
+        nc.vector.tensor_scalar(neg_row[:], max_row[:, 0:P], 1.0, None, ALU.mult, ALU.min, accum_out=neg_max[:])
+        words = keep.tile([P, S], U32, name="words", tag="w1_bf1", align_bytes=64)
         for h in range(halves):
             nc.vector.tensor_copy(words[:, h * BANK : (h + 1) * BANK], word_table[:].indirect(lists[h]))
 

@@ -21,8 +21,8 @@ ALU = mybir.AluOpType
 ACT = mybir.ActivationFunctionType
 
 SCORE_ROW = P - 1
-SCALE_ROW = P - 16
-ZERO_SPLIT = 2048
+SCALE_ROW = 48
+ZERO_SPLIT = 1920
 PIECES = (256, 256, 256, 128, 128)
 SCALAR_WEAVES = (0, 0, 64, 128, 128)
 LAST_BANK = 5
@@ -44,7 +44,7 @@ def tile_picked_ygcb_none_p_kernel(tc, x_words, x_scales, w1, w2, score, offs, o
         score_table = keep.tile([P, T], F32, name="score_table", tag="score_table", align_bytes=64)
         nc.sync.dma_start(score_table[SCORE_ROW:P, :], score[0:1, :])
         scale_table = keep.tile([P, T // 4], I32, name="scale_table", tag="scale_table", align_bytes=64)
-        nc.sync.dma_start(scale_table[SCALE_ROW:P, :], x_scales[0].bitcast(I32))
+        nc.sync.dma_start(scale_table[SCALE_ROW : SCALE_ROW + 16, :], x_scales[0].bitcast(I32))
         w1_raw = keep.tile([P, PACK, H], F32, name="w1_raw", tag="w1_raw")
         nc.sync.dma_start(w1_raw[:], w1.rearrange("(p j) c -> p j c", j=PACK))
         word_table = keep.tile([P, T], U32, name="word_table", align_bytes=64)
@@ -54,9 +54,10 @@ def tile_picked_ygcb_none_p_kernel(tc, x_words, x_scales, w1, w2, score, offs, o
         nc.vector.memset(score_table[0:SCORE_ROW, ZERO_SPLIT : T - 1], 0.0)
         nc.vector.memset(score_table[0:SCORE_ROW, T - 1 : T], 0.0)
 
+        nc.gpsimd.memset(scale_table[0:SCALE_ROW, :], 0)
+        nc.gpsimd.memset(scale_table[SCALE_ROW + 16 : P, :], 0)
         ident = keep.tile([P, P], F32, name="ident")
         make_identity(nc, ident[:])
-        nc.gpsimd.memset(scale_table[0:SCALE_ROW, :], 0)
         picked_scales = keep.tile([P, S], U8, name="picked_scales", align_bytes=64)
         nc.gpsimd.memset(picked_scales[:].bitcast(I32), 0)
         minus_one = keep.tile([P, 1], F32, name="minus_one")

@@ -1,7 +1,6 @@
 from contextlib import ExitStack
 
 import concourse.mybir as mybir
-from concourse.masks import make_identity
 
 K, T, S, H, N = 512, 4096, 1024, 512, 256
 P = 128
@@ -34,6 +33,7 @@ def tile_picked_ygcb_none_p_kernel(tc, x_words, x_scales, w1, w2, score, offs, o
     blocks = S // P
     with ExitStack() as ctx:
         keep = ctx.enter_context(tc.tile_pool(name="keep", bufs=1))
+        reuse = ctx.enter_context(tc.tile_pool(name="reuse", bufs=1))
         psum = ctx.enter_context(tc.psum_pool(name="psum", bufs=1))
 
         def bank(b, name):
@@ -43,21 +43,25 @@ def tile_picked_ygcb_none_p_kernel(tc, x_words, x_scales, w1, w2, score, offs, o
         nc.sync.dma_start(offsets[:], offs)
         score_table = keep.tile([P, T], F32, name="score_table", tag="score_table", align_bytes=64)
         nc.sync.dma_start(score_table[SCORE_ROW:P, :], score[0:1, :])
-        scale_table = keep.tile([P, T // 4], I32, name="scale_table", tag="scale_table", align_bytes=64)
+        scale_table = reuse.tile([P, T // 4], I32, name="scale_table", align_bytes=64, offset=0)
         nc.sync.dma_start(scale_table[SCALE_ROW : SCALE_ROW + 16, :], x_scales[0].bitcast(I32))
         w1_raw = keep.tile([P, PACK, H], F32, name="w1_raw", tag="w1_raw")
         nc.sync.dma_start(w1_raw[:], w1.rearrange("(p j) c -> p j c", j=PACK))
         word_table = keep.tile([P, T], U32, name="word_table", align_bytes=64)
         nc.sync.dma_start(word_table[:].bitcast(I32), x_words[0].rearrange("p n t -> p (n t)").bitcast(I32))
 
+        apart = keep.tile([P, P], F32, name="apart")
+        nc.gpsimd.iota(apart[:], [[-1, P]], base=0, channel_multiplier=1, allow_small_or_imprecise_dtypes=True)
+        distance = keep.tile([P, P], F32, name="distance")
+        nc.scalar.activation(distance[:], apart[:], ACT.Abs)
+        ident = keep.tile([P, P], F32, name="ident")
+        nc.scalar.activation(ident[:], distance[:], ACT.Relu, bias=1.0, scale=-1.0)
         nc.gpsimd.memset(score_table[0:SCORE_ROW, 0:ZERO_SPLIT], 0.0)
         nc.vector.memset(score_table[0:SCORE_ROW, ZERO_SPLIT : T - 1], 0.0)
         nc.vector.memset(score_table[0:SCORE_ROW, T - 1 : T], 0.0)
 
         nc.gpsimd.memset(scale_table[0:SCALE_ROW, :], 0)
         nc.gpsimd.memset(scale_table[SCALE_ROW + 16 : P, :], 0)
-        ident = keep.tile([P, P], F32, name="ident")
-        make_identity(nc, ident[:])
         picked_scales = keep.tile([P, S], U8, name="picked_scales", align_bytes=64)
         nc.gpsimd.memset(picked_scales[:].bitcast(I32), 0)
         minus_one = keep.tile([P, 1], F32, name="minus_one")
@@ -89,7 +93,7 @@ def tile_picked_ygcb_none_p_kernel(tc, x_words, x_scales, w1, w2, score, offs, o
             for m0 in range(0, P, share):
                 nc.scalar.copy(cast[:, :, m0 : m0 + share, :].rearrange("p t m j -> p m j t"), columns[:, m0 : m0 + share, :, 2 * g : 2 * g + 2])
             w1_bf.append(cast)
-        neg_cols = keep.tile([P, blocks], F32, name="neg_cols")
+        neg_cols = reuse.tile([P, blocks], F32, name="neg_cols", align_bytes=64, offset=0)
         neg_col_max = keep.tile([P, 1], F32, name="neg_col_max", tag="w2_raw")
         max_row = bank(3, "max_row")
         nc.vector.tensor_scalar(neg_cols[:], turned[:, SCORE_ROW : SCORE_ROW + 2 * blocks : 2], -1.0, None, ALU.mult, ALU.min, accum_out=neg_col_max[:])
@@ -102,7 +106,7 @@ def tile_picked_ygcb_none_p_kernel(tc, x_words, x_scales, w1, w2, score, offs, o
                 nc.tensor.transpose(sp[:, b * P : (b + 1) * P], neg_cols[:, c : c + 1].to_broadcast([P, P]), ident[:])
             spread.append(sp)
 
-        w1_codes = keep.tile([P, H], U32, name="w1_codes", align_bytes=64)
+        w1_codes = reuse.tile([P, H], U32, name="w1_codes", align_bytes=64, offset=64)
         w1_scales = keep.tile([P, H], U8, name="w1_scales", align_bytes=64)
         for g in range(pairs):
             cols = slice(2 * g * P, 2 * (g + 1) * P)

@@ -42,7 +42,8 @@ def tile_picked_ygcb_none_p_kernel(tc, x_words, x_scales, w1, w2, score, offs, o
         offsets = keep.tile([P, S // 16], U16, name="offsets")
         nc.sync.dma_start(offsets[:], offs)
         score_table = keep.tile([P, T], F32, name="score_table", tag="score_table", align_bytes=64)
-        nc.sync.dma_start(score_table[SCORE_ROW:P, :], score[0:1, :])
+        half_rows = score.rearrange("r c -> (r c)")[0 : 3 * T].rearrange("(a x) -> a x", a=2)[:, 0 : T // 2]
+        nc.sync.dma_start(score_table[SCORE_ROW:P, :].rearrange("p (a x) -> p a x", a=2), half_rows.unsqueeze(0))
         scale_table = reuse.tile([P, T // 4], I32, name="scale_table", align_bytes=64, offset=0)
         nc.sync.dma_start(scale_table[SCALE_ROW : SCALE_ROW + 16, :], x_scales[0].bitcast(I32))
         w1_raw = keep.tile([P, PACK, H], F32, name="w1_raw", tag="w1_raw")
@@ -94,7 +95,7 @@ def tile_picked_ygcb_none_p_kernel(tc, x_words, x_scales, w1, w2, score, offs, o
                 nc.scalar.copy(cast[:, :, m0 : m0 + share, :].rearrange("p t m j -> p m j t"), columns[:, m0 : m0 + share, :, 2 * g : 2 * g + 2])
             w1_bf.append(cast)
         neg_cols = reuse.tile([P, blocks], F32, name="neg_cols", align_bytes=64, offset=0)
-        neg_col_max = keep.tile([P, 1], F32, name="neg_col_max", tag="w2_raw")
+        neg_col_max = keep.tile([P, 1], F32, name="neg_col_max")
         max_row = bank(3, "max_row")
         nc.vector.tensor_scalar(neg_cols[:], turned[:, SCORE_ROW : SCORE_ROW + 2 * blocks : 2], -1.0, None, ALU.mult, ALU.min, accum_out=neg_col_max[:])
         nc.tensor.transpose(max_row[:, 0:P], neg_col_max[:].to_broadcast([P, P]), ident[:])
@@ -128,7 +129,7 @@ def tile_picked_ygcb_none_p_kernel(tc, x_words, x_scales, w1, w2, score, offs, o
         inv_total = keep.tile([P, 1], F32, name="inv_total")
         nc.gpsimd.tensor_tensor(inv_total[:], total[:], minus_one[:], ALU.pow)
 
-        w2_raw = keep.tile([P, PACK, N], F32, name="w2_raw", tag="w2_raw")
+        w2_raw = keep.tile([P, PACK, N], F32, name="w2_raw", tag="w1_bf0", align_bytes=64)
         nc.sync.dma_start(w2_raw[:], w2.rearrange("(p j) c -> p j c", j=PACK))
         w2_bf = keep.tile([P, N, PACK], BF16, name="w2_bf", tag="w2_bf", align_bytes=64)
         nc.scalar.copy(

@@ -21,10 +21,11 @@ ACT = mybir.ActivationFunctionType
 
 SCORE_ROW = P - 1
 SCALE_ROW = 48
-ZERO_SPLIT = 1920
+ZERO_CUTS = (1920, 3839)
 PIECES = (256, 256, 256, 128, 128)
 SCALAR_WEAVES = (0, 0, 64, 128, 128)
 LAST_BANK = 5
+RUN = 8
 
 
 def tile_picked_ygcb_none_p_kernel(tc, x_words, x_scales, w1, w2, score, offs, out):
@@ -33,36 +34,37 @@ def tile_picked_ygcb_none_p_kernel(tc, x_words, x_scales, w1, w2, score, offs, o
     blocks = S // P
     with ExitStack() as ctx:
         keep = ctx.enter_context(tc.tile_pool(name="keep", bufs=1))
-        reuse = ctx.enter_context(tc.tile_pool(name="reuse", bufs=1))
         psum = ctx.enter_context(tc.psum_pool(name="psum", bufs=1))
 
         def bank(b, name):
             return psum.tile([P, BANK], F32, name=name, tag="bank%d" % b)
 
-        offsets = keep.tile([P, S // 16], U16, name="offsets")
-        nc.sync.dma_start(offsets[:], offs)
-        score_table = keep.tile([P, T], F32, name="score_table", tag="score_table", align_bytes=64)
+        score_table = keep.tile([P, T], F32, name="score_table", align_bytes=64)
         half_rows = score.rearrange("r c -> (r c)")[0 : 3 * T].rearrange("(a x) -> a x", a=2)[:, 0 : T // 2]
         nc.sync.dma_start(score_table[SCORE_ROW:P, :].rearrange("p (a x) -> p a x", a=2), half_rows.unsqueeze(0))
-        scale_table = reuse.tile([P, T // 4], I32, name="scale_table", align_bytes=64, offset=0)
+        offsets = keep.tile([P, S // 16], U16, name="offsets")
+        nc.sync.dma_start(offsets[:], offs)
+        scale_table = keep.tile([P, T // 4], I32, name="scale_table", align_bytes=64)
         nc.sync.dma_start(scale_table[SCALE_ROW : SCALE_ROW + 16, :], x_scales[0].bitcast(I32))
-        w1_raw = keep.tile([P, PACK, H], F32, name="w1_raw", tag="w1_raw")
-        nc.sync.dma_start(w1_raw[:], w1.rearrange("(p j) c -> p j c", j=PACK))
         word_table = keep.tile([P, T], U32, name="word_table", align_bytes=64)
         nc.sync.dma_start(word_table[:].bitcast(I32), x_words[0].rearrange("p n t -> p (n t)").bitcast(I32))
+        w1_raw = keep.tile([P, PACK, H], F32, name="w1_raw", align_bytes=64)
+        nc.sync.dma_start(w1_raw[:], w1.rearrange("(p j) c -> p j c", j=PACK))
 
+        zero = keep.tile([P, 1], F32, name="zero")
+        nc.gpsimd.memset(zero[:], 0.0)
         apart = keep.tile([P, P], F32, name="apart")
         nc.gpsimd.iota(apart[:], [[-1, P]], base=0, channel_multiplier=1, allow_small_or_imprecise_dtypes=True)
-        distance = keep.tile([P, P], F32, name="distance")
-        nc.scalar.activation(distance[:], apart[:], ACT.Abs)
         ident = keep.tile([P, P], F32, name="ident")
-        nc.scalar.activation(ident[:], distance[:], ACT.Relu, bias=1.0, scale=-1.0)
-        nc.gpsimd.memset(score_table[0:SCORE_ROW, 0:ZERO_SPLIT], 0.0)
-        nc.vector.memset(score_table[0:SCORE_ROW, ZERO_SPLIT : T - 1], 0.0)
-        nc.vector.memset(score_table[0:SCORE_ROW, T - 1 : T], 0.0)
-
+        nc.vector.tensor_tensor(ident[:], apart[:], zero[:].to_broadcast([P, P]), ALU.is_equal)
+        first_cut, second_cut = ZERO_CUTS
+        nc.gpsimd.memset(score_table[0:SCORE_ROW, 0:first_cut], 0.0)
+        nc.vector.memset(score_table[0:SCORE_ROW, first_cut:second_cut], 0.0)
+        nc.scalar.copy(score_table[0:SCORE_ROW, second_cut:T], zero[0:SCORE_ROW, :].to_broadcast([SCORE_ROW, T - second_cut]))
+        last = T // 4 - 1
         nc.gpsimd.memset(scale_table[0:SCALE_ROW, :], 0)
-        nc.gpsimd.memset(scale_table[SCALE_ROW + 16 : P, :], 0)
+        nc.vector.memset(scale_table[SCALE_ROW + 16 : P, 0:last], 0)
+        nc.vector.memset(scale_table[SCALE_ROW + 16 : P, last : last + 1], 0)
         picked_scales = keep.tile([P, S], U8, name="picked_scales", align_bytes=64)
         nc.gpsimd.memset(picked_scales[:].bitcast(I32), 0)
         minus_one = keep.tile([P, 1], F32, name="minus_one")
@@ -72,32 +74,27 @@ def tile_picked_ygcb_none_p_kernel(tc, x_words, x_scales, w1, w2, score, offs, o
         cols16 = BANK // 16
         lists = [offsets[:, h * cols16 : (h + 1) * cols16] for h in range(halves)]
         turned = bank(6, "turned")
-        picked_score = keep.tile([P, S], F32, name="picked_score", align_bytes=64)
         for h in range(halves):
-            nc.vector.tensor_copy(picked_score[:, h * BANK : (h + 1) * BANK], score_table[:].indirect(lists[h]))
+            picked_score = keep.tile([P, BANK], F32, name="picked_score%d" % h, align_bytes=64)
+            nc.scalar.activation(picked_score[:], score_table[:].indirect(lists[h]), ACT.Copy)
             for b in range(per_bank):
-                c = h * per_bank + b
-                left = 2 * (blocks - 1 - c)
-                nc.tensor.transpose(turned[:, left : left + P], picked_score[:, c * P : (c + 1) * P], ident[:])
+                left = 2 * (blocks - 1 - (h * per_bank + b))
+                nc.tensor.transpose(turned[:, left : left + P], picked_score[:, b * P : (b + 1) * P], ident[:])
 
         apart_scales = keep.tile([P, S], U8, name="apart_scales", align_bytes=64)
         nc.vector.tensor_copy(apart_scales[:], scale_table[:].bitcast(U8).indirect(offsets[:]))
         for q in range(4):
             nc.sync.dma_start(picked_scales[32 * q : 32 * q + 4, :].bitcast(I32), apart_scales[SCALE_ROW + 4 * q : SCALE_ROW + 4 * q + 4, :].bitcast(I32))
+        w2_raw = keep.tile([P, PACK, N], F32, name="w2_raw", tag="scale_table", align_bytes=64)
+        w2_rows = w2.rearrange("(b t r) c -> t b r c", t=PACK, r=RUN)
+        for t in range(PACK):
+            nc.sync.dma_start(w2_raw[:, t, :], w2_rows[t])
 
-        pairs = PACK // 2
-        share = P // 2
-        w1_bf = []
-        for g in range(pairs):
-            cast = keep.tile([P, 2, P, PACK], BF16, name="w1_bf%d" % g, align_bytes=64)
-            columns = w1_raw[:].rearrange("p j (m t) -> p m j t", t=PACK)
-            for m0 in range(0, P, share):
-                nc.scalar.copy(cast[:, :, m0 : m0 + share, :].rearrange("p t m j -> p m j t"), columns[:, m0 : m0 + share, :, 2 * g : 2 * g + 2])
-            w1_bf.append(cast)
-        neg_cols = reuse.tile([P, blocks], F32, name="neg_cols", align_bytes=64, offset=0)
-        neg_col_max = keep.tile([P, 1], F32, name="neg_col_max")
+        neg_cols = keep.tile([P, blocks], F32, name="neg_cols", align_bytes=64)
+        neg_col_max = keep.tile([P, 1], F32, name="neg_col_max", align_bytes=64)
         max_row = bank(3, "max_row")
-        nc.vector.tensor_scalar(neg_cols[:], turned[:, SCORE_ROW : SCORE_ROW + 2 * blocks : 2], -1.0, None, ALU.mult, ALU.min, accum_out=neg_col_max[:])
+        nc.scalar.activation(neg_cols[:], turned[:, SCORE_ROW : SCORE_ROW + 2 * blocks : 2], ACT.Copy, scale=-1.0)
+        nc.vector.tensor_reduce(neg_col_max[:], neg_cols[:], mybir.AxisListType.X, ALU.min)
         nc.tensor.transpose(max_row[:, 0:P], neg_col_max[:].to_broadcast([P, P]), ident[:])
         spread = []
         for h in range(halves):
@@ -106,17 +103,11 @@ def tile_picked_ygcb_none_p_kernel(tc, x_words, x_scales, w1, w2, score, offs, o
                 c = blocks - 1 - (h * per_bank + b)
                 nc.tensor.transpose(sp[:, b * P : (b + 1) * P], neg_cols[:, c : c + 1].to_broadcast([P, P]), ident[:])
             spread.append(sp)
-
-        w1_codes = reuse.tile([P, H], U32, name="w1_codes", align_bytes=64, offset=64)
-        w1_scales = keep.tile([P, H], U8, name="w1_scales", align_bytes=64)
-        for g in range(pairs):
-            cols = slice(2 * g * P, 2 * (g + 1) * P)
-            nc.vector.quantize_mx(w1_codes[:, cols].bitcast(FP8X4), w1_scales[:, cols], w1_bf[g][:].rearrange("p t m j -> p (t m j)"))
-
-        neg_row = keep.tile([P, P], F32, name="neg_row", tag="w1_bf0", align_bytes=64)
-        neg_max = keep.tile([P, 1], F32, name="neg_max", tag="w2_bf", align_bytes=64)
+        neg_row = keep.tile([P, P], F32, name="neg_row", align_bytes=64)
+        neg_max = keep.tile([P, 1], F32, name="neg_max", align_bytes=64)
         nc.vector.tensor_scalar(neg_row[:], max_row[:, 0:P], 1.0, None, ALU.mult, ALU.min, accum_out=neg_max[:])
-        words = keep.tile([P, S], U32, name="words", tag="w1_bf1", align_bytes=64)
+
+        words = keep.tile([P, S], U32, name="words", tag="neg_col_max", align_bytes=64)
         for h in range(halves):
             nc.vector.tensor_copy(words[:, h * BANK : (h + 1) * BANK], word_table[:].indirect(lists[h]))
 
@@ -129,9 +120,20 @@ def tile_picked_ygcb_none_p_kernel(tc, x_words, x_scales, w1, w2, score, offs, o
         inv_total = keep.tile([P, 1], F32, name="inv_total")
         nc.gpsimd.tensor_tensor(inv_total[:], total[:], minus_one[:], ALU.pow)
 
-        w2_raw = keep.tile([P, PACK, N], F32, name="w2_raw", tag="w1_bf0", align_bytes=64)
-        nc.sync.dma_start(w2_raw[:], w2.rearrange("(p j) c -> p j c", j=PACK))
-        w2_bf = keep.tile([P, N, PACK], BF16, name="w2_bf", tag="w2_bf", align_bytes=64)
+        w1_planes = keep.tile([P, PACK, P, PACK], BF16, name="w1_planes", tag="neg_cols", align_bytes=64)
+        w1_bf = [w1_planes[:, t] for t in range(PACK)]
+        columns = w1_raw[:].rearrange("p j (b t h i) -> p t b h j i", t=PACK, h=RUN // 4, i=4)
+        for t, copy in ((0, nc.scalar.copy), (2, nc.vector.tensor_copy), (1, nc.scalar.copy), (3, nc.scalar.copy)):
+            copy(w1_bf[t].rearrange("p (b h i) j -> p b h j i", h=RUN // 4, i=4), columns[:, t])
+        w1_codes, w1_scales = [], []
+        for t in range(PACK):
+            codes = keep.tile([P, P], U32, name="w1_codes%d" % t, align_bytes=64)
+            scales = keep.tile([P, P], U8, name="w1_scales%d" % t, align_bytes=64)
+            nc.vector.quantize_mx(codes[:].bitcast(FP8X4), scales[:], w1_bf[t].rearrange("p m j -> p (m j)"))
+            w1_codes.append(codes)
+            w1_scales.append(scales)
+
+        w2_bf = keep.tile([P, N, PACK], BF16, name="w2_bf", tag="w1_raw", align_bytes=64)
         nc.scalar.copy(
             w2_bf[:].rearrange("p (c i) j -> p c j i", i=4),
             w2_raw[:].rearrange("p j (c i) -> p c j i", i=4),
@@ -139,9 +141,8 @@ def tile_picked_ygcb_none_p_kernel(tc, x_words, x_scales, w1, w2, score, offs, o
 
         starts = [sum(PIECES[:q]) for q in range(len(PIECES))]
         part_ctx = keep.tile([P, PACK * halves], F32, name="part_ctx")
-        z_planes = keep.tile([P, PACK, S], BF16, name="z_planes", align_bytes=64)
+        z_planes = keep.tile([P, PACK, S], BF16, name="z_planes", tag="scale_table", align_bytes=64)
         for t in range(PACK):
-            cols = slice(t * P, (t + 1) * P)
             y = []
             for h in range(halves):
                 js = slice(h * BANK, (h + 1) * BANK)
@@ -149,8 +150,8 @@ def tile_picked_ygcb_none_p_kernel(tc, x_words, x_scales, w1, w2, score, offs, o
                 yb = bank(u, "y%d" % u)
                 nc.tensor.matmul_mx(
                     yb[:],
-                    lhsT=w1_codes[:, cols].bitcast(FP8X4),
-                    lhsT_scale=w1_scales[:, cols],
+                    lhsT=w1_codes[t][:].bitcast(FP8X4),
+                    lhsT_scale=w1_scales[t][:],
                     rhs=words[:, js].bitcast(FP8X4),
                     rhs_scale=picked_scales[:, js],
                     start=True,
@@ -173,18 +174,6 @@ def tile_picked_ygcb_none_p_kernel(tc, x_words, x_scales, w1, w2, score, offs, o
             for c0, c1 in zip(cuts, cuts[1:]):
                 h = c0 // BANK
                 nc.scalar.activation(z_planes[:, t, c0:c1], y[h][:, c0 - h * BANK : c1 - h * BANK], ACT.Identity, bias=context[:])
-
-        for b in (5, 6, 7,):
-            idle = bank(b, "idle%d" % b)
-            nc.tensor.matmul_mx(
-                idle[:],
-                lhsT=w1_codes[:, 0:P].bitcast(FP8X4),
-                lhsT_scale=w1_scales[:, 0:P],
-                rhs=words[:, 0:BANK].bitcast(FP8X4),
-                rhs_scale=picked_scales[:, 0:BANK],
-                start=True,
-                stop=True,
-            )
 
         w2_codes, w2_scales = [], []
         for g in range(N // P):

@@ -21,7 +21,8 @@ ACT = mybir.ActivationFunctionType
 
 SCORE_ROW = P - 1
 SCALE_ROW = 48
-ZERO_CUTS = (1920, 3839)
+ZERO_SPLIT = 4032
+CAST_CUT = 10
 PIECES = (256, 256, 256, 128, 128)
 SCALAR_WEAVES = (0, 0, 64, 128, 128)
 LAST_BANK = 5
@@ -57,18 +58,14 @@ def tile_picked_ygcb_none_p_kernel(tc, x_words, x_scales, w1, w2, score, offs, o
         nc.gpsimd.iota(apart[:], [[-1, P]], base=0, channel_multiplier=1, allow_small_or_imprecise_dtypes=True)
         ident = keep.tile([P, P], F32, name="ident")
         nc.vector.tensor_tensor(ident[:], apart[:], zero[:].to_broadcast([P, P]), ALU.is_equal)
-        first_cut, second_cut = ZERO_CUTS
-        nc.gpsimd.memset(score_table[0:SCORE_ROW, 0:first_cut], 0.0)
-        nc.vector.memset(score_table[0:SCORE_ROW, first_cut:second_cut], 0.0)
-        nc.scalar.copy(score_table[0:SCORE_ROW, second_cut:T], zero[0:SCORE_ROW, :].to_broadcast([SCORE_ROW, T - second_cut]))
-        last = T // 4 - 1
-        nc.gpsimd.memset(scale_table[0:SCALE_ROW, :], 0)
-        nc.vector.memset(scale_table[SCALE_ROW + 16 : P, 0:last], 0)
-        nc.vector.memset(scale_table[SCALE_ROW + 16 : P, last : last + 1], 0)
-        picked_scales = keep.tile([P, S], U8, name="picked_scales", align_bytes=64)
-        nc.gpsimd.memset(picked_scales[:].bitcast(I32), 0)
         minus_one = keep.tile([P, 1], F32, name="minus_one")
         nc.gpsimd.memset(minus_one[:], -1.0)
+        picked_scales = keep.tile([P, S], U8, name="picked_scales", align_bytes=64)
+        nc.gpsimd.memset(picked_scales[:].bitcast(I32), 0)
+        nc.vector.memset(score_table[0:SCORE_ROW, 0:ZERO_SPLIT], 0.0)
+        nc.scalar.copy(score_table[0:SCORE_ROW, ZERO_SPLIT:T], zero[0:SCORE_ROW, :].to_broadcast([SCORE_ROW, T - ZERO_SPLIT]))
+        nc.vector.memset(scale_table[0:SCALE_ROW, :], 0)
+        nc.vector.memset(scale_table[SCALE_ROW + 16 : P, :], 0)
 
         per_bank = BANK // P
         cols16 = BANK // 16
@@ -93,8 +90,7 @@ def tile_picked_ygcb_none_p_kernel(tc, x_words, x_scales, w1, w2, score, offs, o
         neg_cols = keep.tile([P, blocks], F32, name="neg_cols", align_bytes=64)
         neg_col_max = keep.tile([P, 1], F32, name="neg_col_max", align_bytes=64)
         max_row = bank(3, "max_row")
-        nc.scalar.activation(neg_cols[:], turned[:, SCORE_ROW : SCORE_ROW + 2 * blocks : 2], ACT.Copy, scale=-1.0)
-        nc.vector.tensor_reduce(neg_col_max[:], neg_cols[:], mybir.AxisListType.X, ALU.min)
+        nc.vector.tensor_scalar(neg_cols[:], turned[:, SCORE_ROW : SCORE_ROW + 2 * blocks : 2], -1.0, None, ALU.mult, ALU.min, accum_out=neg_col_max[:])
         nc.tensor.transpose(max_row[:, 0:P], neg_col_max[:].to_broadcast([P, P]), ident[:])
         spread = []
         for h in range(halves):
@@ -123,8 +119,16 @@ def tile_picked_ygcb_none_p_kernel(tc, x_words, x_scales, w1, w2, score, offs, o
         w1_planes = keep.tile([P, PACK, P, PACK], BF16, name="w1_planes", tag="neg_cols", align_bytes=64)
         w1_bf = [w1_planes[:, t] for t in range(PACK)]
         columns = w1_raw[:].rearrange("p j (b t h i) -> p t b h j i", t=PACK, h=RUN // 4, i=4)
-        for t, copy in ((0, nc.scalar.copy), (2, nc.vector.tensor_copy), (1, nc.scalar.copy), (3, nc.scalar.copy)):
-            copy(w1_bf[t].rearrange("p (b h i) j -> p b h j i", h=RUN // 4, i=4), columns[:, t])
+        runs = P // RUN
+        shares = (
+            (nc.vector.tensor_copy, 0, 0, runs),
+            (nc.vector.tensor_copy, 1, 0, CAST_CUT),
+            (nc.scalar.copy, 1, CAST_CUT, runs),
+            (nc.scalar.copy, 2, 0, runs),
+            (nc.scalar.copy, 3, 0, runs),
+        )
+        for copy, t, b0, b1 in shares:
+            copy(w1_bf[t].rearrange("p (b h i) j -> p b h j i", h=RUN // 4, i=4)[:, b0:b1], columns[:, t, b0:b1])
         w1_codes, w1_scales = [], []
         for t in range(PACK):
             codes = keep.tile([P, P], U32, name="w1_codes%d" % t, align_bytes=64)

@@ -83,9 +83,9 @@ def tile_picked_ygcb_none_p_kernel(tc, x_words, x_scales, w1, w2, score, offs, o
         for q in range(4):
             nc.sync.dma_start(picked_scales[32 * q : 32 * q + 4, :].bitcast(I32), apart_scales[SCALE_ROW + 4 * q : SCALE_ROW + 4 * q + 4, :].bitcast(I32))
         w2_raw = keep.tile([P, PACK, N], F32, name="w2_raw", tag="scale_table", align_bytes=64)
-        w2_rows = w2.rearrange("(b t r) c -> t b r c", t=PACK, r=RUN)
-        for t in range(PACK):
-            nc.sync.dma_start(w2_raw[:, t, :], w2_rows[t])
+        w2_rows = w2.rearrange("(b u r e) c -> u b r (e c)", u=2, r=RUN, e=2)
+        for u in range(2):
+            nc.sync.dma_start(w2_raw[:, 2 * u : 2 * u + 2, :].rearrange("p e c -> p (e c)"), w2_rows[u])
 
         neg_cols = keep.tile([P, blocks], F32, name="neg_cols", align_bytes=64)
         neg_col_max = keep.tile([P, 1], F32, name="neg_col_max", align_bytes=64)
@@ -118,7 +118,7 @@ def tile_picked_ygcb_none_p_kernel(tc, x_words, x_scales, w1, w2, score, offs, o
 
         w1_planes = keep.tile([P, PACK, P, PACK], BF16, name="w1_planes", tag="neg_cols", align_bytes=64)
         w1_bf = [w1_planes[:, t] for t in range(PACK)]
-        columns = w1_raw[:].rearrange("p j (b t h i) -> p t b h j i", t=PACK, h=RUN // 4, i=4)
+        columns = w1_raw[:].rearrange("p j (b u h i e) -> p u e b h j i", u=2, h=RUN // 2, i=2, e=2)
         runs = P // RUN
         shares = (
             (nc.vector.tensor_copy, 0, 0, runs),
@@ -128,7 +128,7 @@ def tile_picked_ygcb_none_p_kernel(tc, x_words, x_scales, w1, w2, score, offs, o
             (nc.scalar.copy, 3, 0, runs),
         )
         for copy, t, b0, b1 in shares:
-            copy(w1_bf[t].rearrange("p (b h i) j -> p b h j i", h=RUN // 4, i=4)[:, b0:b1], columns[:, t, b0:b1])
+            copy(w1_bf[t].rearrange("p (b h i) j -> p b h j i", h=RUN // 2, i=2)[:, b0:b1], columns[:, t // 2, t % 2, b0:b1])
         w1_codes, w1_scales = [], []
         for t in range(PACK):
             codes = keep.tile([P, P], U32, name="w1_codes%d" % t, align_bytes=64)

@@ -21,12 +21,12 @@ ACT = mybir.ActivationFunctionType
 
 SCORE_ROW = P - 1
 SCALE_ROW = 48
-ZERO_SPLIT = 4032
 CAST_CUT = 10
 PIECES = (256, 256, 256, 128, 128)
 SCALAR_WEAVES = (0, 0, 64, 128, 128)
 LAST_BANK = 5
 RUN = 8
+ZERO_SPLIT = 4032
 
 
 def tile_picked_ygcb_none_p_kernel(tc, x_words, x_scales, w1, w2, score, offs, out):
@@ -52,20 +52,25 @@ def tile_picked_ygcb_none_p_kernel(tc, x_words, x_scales, w1, w2, score, offs, o
         w1_raw = keep.tile([P, PACK, H], F32, name="w1_raw", align_bytes=64)
         nc.sync.dma_start(w1_raw[:], w1.rearrange("(p j) c -> p j c", j=PACK))
 
+        w2_raw = keep.tile([P, PACK, N], F32, name="w2_raw", align_bytes=64)
+        w2_rows = w2.rearrange("(b u r e) c -> u b r (e c)", u=2, r=RUN, e=2)
+        for u in range(2):
+            nc.sync.dma_start(w2_raw[:, 2 * u : 2 * u + 2, :].rearrange("p e c -> p (e c)"), w2_rows[u])
+
         zero = keep.tile([P, 1], F32, name="zero")
         nc.gpsimd.memset(zero[:], 0.0)
         apart = keep.tile([P, P], F32, name="apart")
         nc.gpsimd.iota(apart[:], [[-1, P]], base=0, channel_multiplier=1, allow_small_or_imprecise_dtypes=True)
-        ident = keep.tile([P, P], F32, name="ident")
-        nc.vector.tensor_tensor(ident[:], apart[:], zero[:].to_broadcast([P, P]), ALU.is_equal)
-        minus_one = keep.tile([P, 1], F32, name="minus_one")
-        nc.gpsimd.memset(minus_one[:], -1.0)
-        picked_scales = keep.tile([P, S], U8, name="picked_scales", align_bytes=64)
-        nc.gpsimd.memset(picked_scales[:].bitcast(I32), 0)
         nc.vector.memset(score_table[0:SCORE_ROW, 0:ZERO_SPLIT], 0.0)
         nc.scalar.copy(score_table[0:SCORE_ROW, ZERO_SPLIT:T], zero[0:SCORE_ROW, :].to_broadcast([SCORE_ROW, T - ZERO_SPLIT]))
+        ident = keep.tile([P, P], F32, name="ident")
+        nc.vector.tensor_single_scalar(ident[:], apart[:], 0.0, ALU.is_equal)
         nc.vector.memset(scale_table[0:SCALE_ROW, :], 0)
         nc.vector.memset(scale_table[SCALE_ROW + 16 : P, :], 0)
+        picked_scales = keep.tile([P, S], U8, name="picked_scales", align_bytes=64)
+        nc.vector.memset(picked_scales[:].bitcast(I32), 0)
+        minus_one = keep.tile([P, 1], F32, name="minus_one")
+        nc.vector.memset(minus_one[:], -1.0)
 
         per_bank = BANK // P
         cols16 = BANK // 16
@@ -81,11 +86,7 @@ def tile_picked_ygcb_none_p_kernel(tc, x_words, x_scales, w1, w2, score, offs, o
         apart_scales = keep.tile([P, S], U8, name="apart_scales", align_bytes=64)
         nc.vector.tensor_copy(apart_scales[:], scale_table[:].bitcast(U8).indirect(offsets[:]))
         for q in range(4):
-            nc.sync.dma_start(picked_scales[32 * q : 32 * q + 4, :].bitcast(I32), apart_scales[SCALE_ROW + 4 * q : SCALE_ROW + 4 * q + 4, :].bitcast(I32))
-        w2_raw = keep.tile([P, PACK, N], F32, name="w2_raw", tag="scale_table", align_bytes=64)
-        w2_rows = w2.rearrange("(b u r e) c -> u b r (e c)", u=2, r=RUN, e=2)
-        for u in range(2):
-            nc.sync.dma_start(w2_raw[:, 2 * u : 2 * u + 2, :].rearrange("p e c -> p (e c)"), w2_rows[u])
+            nc.scalar.dma_start(picked_scales[32 * q : 32 * q + 4, :].bitcast(I32), apart_scales[SCALE_ROW + 4 * q : SCALE_ROW + 4 * q + 4, :].bitcast(I32))
 
         neg_cols = keep.tile([P, blocks], F32, name="neg_cols", align_bytes=64)
         neg_col_max = keep.tile([P, 1], F32, name="neg_col_max", align_bytes=64)
@@ -101,11 +102,10 @@ def tile_picked_ygcb_none_p_kernel(tc, x_words, x_scales, w1, w2, score, offs, o
             spread.append(sp)
         neg_row = keep.tile([P, P], F32, name="neg_row", align_bytes=64)
         neg_max = keep.tile([P, 1], F32, name="neg_max", align_bytes=64)
+        words = keep.tile([P, S], U32, name="words", align_bytes=64)
+        nc.vector.tensor_copy(words[:, 0:BANK], word_table[:].indirect(lists[0]))
         nc.vector.tensor_scalar(neg_row[:], max_row[:, 0:P], 1.0, None, ALU.mult, ALU.min, accum_out=neg_max[:])
-
-        words = keep.tile([P, S], U32, name="words", tag="neg_col_max", align_bytes=64)
-        for h in range(halves):
-            nc.vector.tensor_copy(words[:, h * BANK : (h + 1) * BANK], word_table[:].indirect(lists[h]))
+        nc.vector.tensor_copy(words[:, BANK:S], word_table[:].indirect(lists[1]))
 
         ee = keep.tile([P, S], F32, name="ee")
         part_total = keep.tile([P, halves], F32, name="part_total")
@@ -145,7 +145,7 @@ def tile_picked_ygcb_none_p_kernel(tc, x_words, x_scales, w1, w2, score, offs, o
 
         starts = [sum(PIECES[:q]) for q in range(len(PIECES))]
         part_ctx = keep.tile([P, PACK * halves], F32, name="part_ctx")
-        z_planes = keep.tile([P, PACK, S], BF16, name="z_planes", tag="scale_table", align_bytes=64)
+        z_planes = keep.tile([P, PACK, S], BF16, name="z_planes", tag="w2_raw", align_bytes=64)
         for t in range(PACK):
             y = []
             for h in range(halves):

@@ -52,10 +52,6 @@ def tile_picked_ygcb_none_p_kernel(tc, x_words, x_scales, w1, w2, score, offs, o
         w1_raw = keep.tile([P, PACK, H], F32, name="w1_raw", align_bytes=64)
         nc.sync.dma_start(w1_raw[:], w1.rearrange("(p j) c -> p j c", j=PACK))
 
-        w2_raw = keep.tile([P, PACK, N], F32, name="w2_raw", align_bytes=64)
-        w2_rows = w2.rearrange("(b u r e) c -> u b r (e c)", u=2, r=RUN, e=2)
-        for u in range(2):
-            nc.sync.dma_start(w2_raw[:, 2 * u : 2 * u + 2, :].rearrange("p e c -> p (e c)"), w2_rows[u])
 
         zero = keep.tile([P, 1], F32, name="zero")
         nc.gpsimd.memset(zero[:], 0.0)
@@ -86,7 +82,11 @@ def tile_picked_ygcb_none_p_kernel(tc, x_words, x_scales, w1, w2, score, offs, o
         apart_scales = keep.tile([P, S], U8, name="apart_scales", align_bytes=64)
         nc.vector.tensor_copy(apart_scales[:], scale_table[:].bitcast(U8).indirect(offsets[:]))
         for q in range(4):
-            nc.scalar.dma_start(picked_scales[32 * q : 32 * q + 4, :].bitcast(I32), apart_scales[SCALE_ROW + 4 * q : SCALE_ROW + 4 * q + 4, :].bitcast(I32))
+            nc.sync.dma_start(picked_scales[32 * q : 32 * q + 4, :].bitcast(I32), apart_scales[SCALE_ROW + 4 * q : SCALE_ROW + 4 * q + 4, :].bitcast(I32))
+        w2_raw = keep.tile([P, PACK, N], F32, name="w2_raw", tag="scale_table", align_bytes=64)
+        w2_rows = w2.rearrange("(b u r e) c -> u b r (e c)", u=2, r=RUN, e=2)
+        for u in range(2):
+            nc.sync.dma_start(w2_raw[:, 2 * u : 2 * u + 2, :].rearrange("p e c -> p (e c)"), w2_rows[u])
 
         neg_cols = keep.tile([P, blocks], F32, name="neg_cols", align_bytes=64)
         neg_col_max = keep.tile([P, 1], F32, name="neg_col_max", align_bytes=64)
@@ -103,9 +103,9 @@ def tile_picked_ygcb_none_p_kernel(tc, x_words, x_scales, w1, w2, score, offs, o
         neg_row = keep.tile([P, P], F32, name="neg_row", align_bytes=64)
         neg_max = keep.tile([P, 1], F32, name="neg_max", align_bytes=64)
         words = keep.tile([P, S], U32, name="words", align_bytes=64)
-        nc.vector.tensor_copy(words[:, 0:BANK], word_table[:].indirect(lists[0]))
         nc.vector.tensor_scalar(neg_row[:], max_row[:, 0:P], 1.0, None, ALU.mult, ALU.min, accum_out=neg_max[:])
-        nc.vector.tensor_copy(words[:, BANK:S], word_table[:].indirect(lists[1]))
+        for h in range(halves):
+            nc.vector.tensor_copy(words[:, h * BANK : (h + 1) * BANK], word_table[:].indirect(lists[h]))
 
         ee = keep.tile([P, S], F32, name="ee")
         part_total = keep.tile([P, halves], F32, name="part_total")
@@ -145,7 +145,7 @@ def tile_picked_ygcb_none_p_kernel(tc, x_words, x_scales, w1, w2, score, offs, o
 
         starts = [sum(PIECES[:q]) for q in range(len(PIECES))]
         part_ctx = keep.tile([P, PACK * halves], F32, name="part_ctx")
-        z_planes = keep.tile([P, PACK, S], BF16, name="z_planes", tag="w2_raw", align_bytes=64)
+        z_planes = keep.tile([P, PACK, S], BF16, name="z_planes", tag="scale_table", align_bytes=64)
         for t in range(PACK):
             y = []
             for h in range(halves):

@@ -21,7 +21,8 @@ ACT = mybir.ActivationFunctionType
 
 SCORE_ROW = P - 1
 SCALE_ROW = 48
-CAST_CUT = 10
+SCORE_PIECE = 256
+PLANE_BYTES = 2 * P * PACK
 PIECES = (256, 256, 256, 128, 128)
 SCALAR_WEAVES = (0, 0, 64, 128, 128)
 LAST_BANK = 5
@@ -35,6 +36,7 @@ def tile_picked_ygcb_none_p_kernel(tc, x_words, x_scales, w1, w2, score, offs, o
     blocks = S // P
     with ExitStack() as ctx:
         keep = ctx.enter_context(tc.tile_pool(name="keep", bufs=1))
+        reuse = ctx.enter_context(tc.tile_pool(name="reuse", bufs=1))
         psum = ctx.enter_context(tc.psum_pool(name="psum", bufs=1))
 
         def bank(b, name):
@@ -72,11 +74,11 @@ def tile_picked_ygcb_none_p_kernel(tc, x_words, x_scales, w1, w2, score, offs, o
         cols16 = BANK // 16
         lists = [offsets[:, h * cols16 : (h + 1) * cols16] for h in range(halves)]
         turned = bank(6, "turned")
-        for h in range(halves):
-            picked_score = keep.tile([P, BANK], F32, name="picked_score%d" % h, align_bytes=64)
-            nc.scalar.activation(picked_score[:], score_table[:].indirect(lists[h]), ACT.Copy)
-            for b in range(per_bank):
-                left = 2 * (blocks - 1 - (h * per_bank + b))
+        for first in range(0, S, SCORE_PIECE):
+            picked_score = keep.tile([P, SCORE_PIECE], F32, name="picked_score%d" % first, align_bytes=64)
+            nc.scalar.activation(picked_score[:], score_table[:].indirect(offsets[:, first // 16 : (first + SCORE_PIECE) // 16]), ACT.Copy)
+            for b in range(SCORE_PIECE // P):
+                left = 2 * (blocks - 1 - (first // P + b))
                 nc.tensor.transpose(turned[:, left : left + P], picked_score[:, b * P : (b + 1) * P], ident[:])
 
         apart_scales = keep.tile([P, S], U8, name="apart_scales", align_bytes=64)
@@ -88,10 +90,11 @@ def tile_picked_ygcb_none_p_kernel(tc, x_words, x_scales, w1, w2, score, offs, o
         for u in range(2):
             nc.sync.dma_start(w2_raw[:, 2 * u : 2 * u + 2, :].rearrange("p e c -> p (e c)"), w2_rows[u])
 
-        neg_cols = keep.tile([P, blocks], F32, name="neg_cols", align_bytes=64)
+        neg_room = reuse.tile([P, 32], F32, name="neg_room", align_bytes=64, offset=PLANE_BYTES - 64)
+        neg_cols = neg_room[:, 0:blocks]
         neg_col_max = keep.tile([P, 1], F32, name="neg_col_max", align_bytes=64)
         max_row = bank(3, "max_row")
-        nc.vector.tensor_scalar(neg_cols[:], turned[:, SCORE_ROW : SCORE_ROW + 2 * blocks : 2], -1.0, None, ALU.mult, ALU.min, accum_out=neg_col_max[:])
+        nc.vector.tensor_scalar(neg_cols, turned[:, SCORE_ROW : SCORE_ROW + 2 * blocks : 2], -1.0, None, ALU.mult, ALU.min, accum_out=neg_col_max[:])
         nc.tensor.transpose(max_row[:, 0:P], neg_col_max[:].to_broadcast([P, P]), ident[:])
         spread = []
         for h in range(halves):
@@ -116,28 +119,31 @@ def tile_picked_ygcb_none_p_kernel(tc, x_words, x_scales, w1, w2, score, offs, o
         inv_total = keep.tile([P, 1], F32, name="inv_total")
         nc.gpsimd.tensor_tensor(inv_total[:], total[:], minus_one[:], ALU.pow)
 
-        w1_planes = keep.tile([P, PACK, P, PACK], BF16, name="w1_planes", tag="neg_cols", align_bytes=64)
-        w1_bf = [w1_planes[:, t] for t in range(PACK)]
         columns = w1_raw[:].rearrange("p j (b u h i e) -> p u e b h j i", u=2, h=RUN // 2, i=2, e=2)
-        runs = P // RUN
-        shares = (
-            (nc.vector.tensor_copy, 0, 0, runs),
-            (nc.vector.tensor_copy, 1, 0, CAST_CUT),
-            (nc.scalar.copy, 1, CAST_CUT, runs),
-            (nc.scalar.copy, 2, 0, runs),
-            (nc.scalar.copy, 3, 0, runs),
-        )
-        for copy, t, b0, b1 in shares:
-            copy(w1_bf[t].rearrange("p (b h i) j -> p b h j i", h=RUN // 2, i=2)[:, b0:b1], columns[:, t // 2, t % 2, b0:b1])
-        w1_codes, w1_scales = [], []
-        for t in range(PACK):
+
+        def cast_plane(copy, t, plane):
+            copy(plane.rearrange("p (b h i) j -> p b h j i", h=RUN // 2, i=2), columns[:, t // 2, t % 2])
+
+        def quantise_plane(t, plane):
             codes = keep.tile([P, P], U32, name="w1_codes%d" % t, align_bytes=64)
             scales = keep.tile([P, P], U8, name="w1_scales%d" % t, align_bytes=64)
-            nc.vector.quantize_mx(codes[:].bitcast(FP8X4), scales[:], w1_bf[t].rearrange("p m j -> p (m j)"))
-            w1_codes.append(codes)
-            w1_scales.append(scales)
+            nc.vector.quantize_mx(codes[:].bitcast(FP8X4), scales[:], plane.rearrange("p m j -> p (m j)"))
+            return codes, scales
 
-        w2_bf = keep.tile([P, N, PACK], BF16, name="w2_bf", tag="w1_raw", align_bytes=64)
+        plane0 = reuse.tile([P, P, PACK], BF16, name="plane0", align_bytes=64, offset=0)
+        odd_planes = reuse.tile([P, 2, P, PACK], BF16, name="odd_planes", align_bytes=64, offset=PLANE_BYTES)
+        cast_plane(nc.vector.tensor_copy, 0, plane0[:])
+        cast_plane(nc.vector.tensor_copy, 1, odd_planes[:, 0])
+        cast_plane(nc.scalar.copy, 3, odd_planes[:, 1])
+        w1_mx = {0: quantise_plane(0, plane0[:]), 1: quantise_plane(1, odd_planes[:, 0])}
+        plane2 = reuse.tile([P, P, PACK], BF16, name="plane2", align_bytes=64, offset=0)
+        cast_plane(nc.vector.tensor_copy, 2, plane2[:])
+        w1_mx[3] = quantise_plane(3, odd_planes[:, 1])
+        w1_mx[2] = quantise_plane(2, plane2[:])
+        w1_codes = [w1_mx[t][0] for t in range(PACK)]
+        w1_scales = [w1_mx[t][1] for t in range(PACK)]
+
+        w2_bf = keep.tile([P, N, PACK], BF16, name="w2_bf", tag="neg_max", align_bytes=64)
         nc.scalar.copy(
             w2_bf[:].rearrange("p (c i) j -> p c j i", i=4),
             w2_raw[:].rearrange("p j (c i) -> p c j i", i=4),

@@ -22,6 +22,7 @@ ACT = mybir.ActivationFunctionType
 SCORE_ROW = P - 1
 SCALE_ROW = 48
 SCORE_PIECE = 256
+VECTOR_RUNS = (6, 10)
 PLANE_BYTES = 2 * P * PACK
 PIECES = (256, 256, 256, 128, 128)
 SCALAR_WEAVES = (0, 0, 64, 128, 128)
@@ -57,8 +58,8 @@ def tile_picked_ygcb_none_p_kernel(tc, x_words, x_scales, w1, w2, score, offs, o
 
         zero = keep.tile([P, 1], F32, name="zero")
         nc.gpsimd.memset(zero[:], 0.0)
-        apart = keep.tile([P, P], F32, name="apart")
-        nc.gpsimd.iota(apart[:], [[-1, P]], base=0, channel_multiplier=1, allow_small_or_imprecise_dtypes=True)
+        apart = keep.tile([P, P], I32, name="apart")
+        nc.gpsimd.iota(apart[:], [[-1, P]], base=0, channel_multiplier=1)
         nc.vector.memset(score_table[0:SCORE_ROW, 0:ZERO_SPLIT], 0.0)
         nc.scalar.copy(score_table[0:SCORE_ROW, ZERO_SPLIT:T], zero[0:SCORE_ROW, :].to_broadcast([SCORE_ROW, T - ZERO_SPLIT]))
         ident = keep.tile([P, P], F32, name="ident")
@@ -68,7 +69,7 @@ def tile_picked_ygcb_none_p_kernel(tc, x_words, x_scales, w1, w2, score, offs, o
         picked_scales = keep.tile([P, S], U8, name="picked_scales", align_bytes=64)
         nc.vector.memset(picked_scales[:].bitcast(I32), 0)
         minus_one = keep.tile([P, 1], F32, name="minus_one")
-        nc.vector.memset(minus_one[:], -1.0)
+        nc.scalar.activation(minus_one[:], zero[:], ACT.Copy, bias=-1.0)
 
         per_bank = BANK // P
         cols16 = BANK // 16
@@ -121,8 +122,9 @@ def tile_picked_ygcb_none_p_kernel(tc, x_words, x_scales, w1, w2, score, offs, o
 
         columns = w1_raw[:].rearrange("p j (b u h i e) -> p u e b h j i", u=2, h=RUN // 2, i=2, e=2)
 
-        def cast_plane(copy, t, plane):
-            copy(plane.rearrange("p (b h i) j -> p b h j i", h=RUN // 2, i=2), columns[:, t // 2, t % 2])
+        def cast_plane(copy, t, plane, b0, b1):
+            rows = plane.rearrange("p (b h i) j -> p b h j i", h=RUN // 2, i=2)
+            copy(rows[:, b0:b1], columns[:, t // 2, t % 2, b0:b1])
 
         def quantise_plane(t, plane):
             codes = keep.tile([P, P], U32, name="w1_codes%d" % t, align_bytes=64)
@@ -132,12 +134,14 @@ def tile_picked_ygcb_none_p_kernel(tc, x_words, x_scales, w1, w2, score, offs, o
 
         plane0 = reuse.tile([P, P, PACK], BF16, name="plane0", align_bytes=64, offset=0)
         odd_planes = reuse.tile([P, 2, P, PACK], BF16, name="odd_planes", align_bytes=64, offset=PLANE_BYTES)
-        cast_plane(nc.vector.tensor_copy, 0, plane0[:])
-        cast_plane(nc.vector.tensor_copy, 1, odd_planes[:, 0])
-        cast_plane(nc.scalar.copy, 3, odd_planes[:, 1])
+        runs = P // RUN
+        for t, plane in ((0, plane0[:]), (1, odd_planes[:, 0])):
+            cast_plane(nc.vector.tensor_copy, t, plane, 0, VECTOR_RUNS[t])
+            cast_plane(nc.scalar.copy, t, plane, VECTOR_RUNS[t], runs)
+        cast_plane(nc.scalar.copy, 3, odd_planes[:, 1], 0, runs)
         w1_mx = {0: quantise_plane(0, plane0[:]), 1: quantise_plane(1, odd_planes[:, 0])}
         plane2 = reuse.tile([P, P, PACK], BF16, name="plane2", align_bytes=64, offset=0)
-        cast_plane(nc.vector.tensor_copy, 2, plane2[:])
+        cast_plane(nc.vector.tensor_copy, 2, plane2[:], 0, runs)
         w1_mx[3] = quantise_plane(3, odd_planes[:, 1])
         w1_mx[2] = quantise_plane(2, plane2[:])
         w1_codes = [w1_mx[t][0] for t in range(PACK)]

@@ -28,7 +28,7 @@ PIECES = (256, 256, 256, 128, 128)
 SCALAR_WEAVES = (0, 0, 64, 128, 128)
 LAST_BANK = 5
 RUN = 8
-ZERO_SPLIT = 4032
+ZERO_SPLIT = 3712
 
 
 def tile_picked_ygcb_none_p_kernel(tc, x_words, x_scales, w1, w2, score, offs, out):

@@ -25,8 +25,8 @@ SCORE_PIECE = 256
 VECTOR_RUNS = (6, 10)
 PLANE_BYTES = 2 * P * PACK
 PIECES = (256, 256, 256, 128, 128)
-SCALAR_WEAVES = (0, 0, 64, 128, 128)
-LAST_BANK = 5
+AT_LAST_SUMS = 3 * PLANE_BYTES
+AT_EARLY = AT_LAST_SUMS + 4 * P
 RUN = 8
 ZERO_SPLIT = 3712
 
@@ -154,10 +154,16 @@ def tile_picked_ygcb_none_p_kernel(tc, x_words, x_scales, w1, w2, score, offs, o
         )
 
         starts = [sum(PIECES[:q]) for q in range(len(PIECES))]
-        part_ctx = keep.tile([P, PACK * halves], F32, name="part_ctx")
-        z_planes = keep.tile([P, PACK, S], BF16, name="z_planes", tag="scale_table", align_bytes=64)
+        z_planes = [
+            keep.tile([P, PACK, BANK], BF16, name="z_planes0", tag="scale_table", align_bytes=64),
+            keep.tile([P, PACK, BANK], BF16, name="z_planes1", tag="w1_raw", align_bytes=64),
+        ]
         for t in range(PACK):
             y = []
+            if t < PACK - 1:
+                part_ctx = keep.tile([P, halves], F32, name="part_ctx%d" % t)
+            else:
+                part_ctx = reuse.tile([P, halves], F32, name="part_ctx%d" % t, align_bytes=64, offset=AT_LAST_SUMS)
             for h in range(halves):
                 js = slice(h * BANK, (h + 1) * BANK)
                 u = t * halves + h
@@ -172,26 +178,24 @@ def tile_picked_ygcb_none_p_kernel(tc, x_words, x_scales, w1, w2, score, offs, o
                     stop=True,
                 )
                 weighted = keep.tile([P, BANK], F32, name="weighted%d" % u, tag="weighted%d" % u, align_bytes=64)
-                factor = 1.0 if t < PACK - 1 else inv_total[:]
-                nc.vector.scalar_tensor_tensor(weighted[:], yb[:], factor, ee[:, js], ALU.mult, ALU.mult, accum_out=part_ctx[:, u : u + 1])
+                nc.vector.scalar_tensor_tensor(weighted[:], yb[:], inv_total[:], ee[:, js], ALU.mult, ALU.mult, accum_out=part_ctx[:, h : h + 1])
                 y.append(yb)
-            u = t * halves
             context = keep.tile([P, 1], F32, name="context%d" % t)
-            first, second = part_ctx[:, u : u + 1], part_ctx[:, u + 1 : u + 2]
+            first, second = part_ctx[:, 0:1], part_ctx[:, 1:2]
+            nc.gpsimd.tensor_tensor(context[:], first, second, ALU.add)
             if t < PACK - 1:
-                nc.gpsimd.tensor_scalar(context[:], first, second, inv_total[:], ALU.add, ALU.mult)
                 cuts = [0, BANK, S]
             else:
-                nc.gpsimd.tensor_tensor(context[:], first, second, ALU.add)
-                nc.vector.tensor_scalar(z_planes[:, t, 0 : PIECES[0]], y[0][:, 0 : PIECES[0]], first, second, ALU.add, ALU.add)
-                cuts = [PIECES[0], BANK, BANK + PIECES[2], S]
+                for c0 in range(0, PIECES[0], P):
+                    nc.vector.tensor_scalar(z_planes[0][:, t, c0 : c0 + P], y[0][:, c0 : c0 + P], first, second, ALU.add, ALU.add)
+                cuts = [PIECES[0], BANK, S]
             for c0, c1 in zip(cuts, cuts[1:]):
                 h = c0 // BANK
-                nc.scalar.activation(z_planes[:, t, c0:c1], y[h][:, c0 - h * BANK : c1 - h * BANK], ACT.Identity, bias=context[:])
+                nc.scalar.activation(z_planes[h][:, t, c0 - h * BANK : c1 - h * BANK], y[h][:, c0 - h * BANK : c1 - h * BANK], ACT.Identity, bias=context[:])
 
         w2_codes, w2_scales = [], []
-        for g in range(N // P):
-            codes = keep.tile([P, P], U32, name="w2_codes%d" % g, tag="weighted%d" % (PACK * halves - 2 + g), align_bytes=64)
+
+        def quantise_w2(g, codes):
             scales = keep.tile([P, P], U8, name="w2_scales%d" % g, align_bytes=64)
             nc.vector.quantize_mx(codes[:].bitcast(FP8X4), scales[:], w2_bf[:, g * P : (g + 1) * P, :].rearrange("p c j -> p (c j)"))
             w2_codes.append(codes)
@@ -199,16 +203,13 @@ def tile_picked_ygcb_none_p_kernel(tc, x_words, x_scales, w1, w2, score, offs, o
 
         groups = N // P
 
-        def weave(q):
-            j0, width = starts[q], PIECES[q]
-            z_bf = keep.tile([P, width, PACK], BF16, name="z_bf%d" % q, align_bytes=64)
-            cut = width - SCALAR_WEAVES[q]
-            for copy, c0, c1 in ((nc.vector.tensor_copy, 0, cut), (nc.scalar.copy, cut, width)):
-                if c1 > c0:
-                    copy(
-                        z_bf[:, c0:c1, :].rearrange("p (c i) t -> p c t i", i=4),
-                        z_planes[:, :, j0 + c0 : j0 + c1].rearrange("p t (c i) -> p c t i", i=4),
-                    )
+        def weave(q, copy, step, z_bf):
+            h, j0 = divmod(starts[q], BANK)
+            for c0 in range(0, PIECES[q], step):
+                copy(
+                    z_bf[:, c0 : c0 + step, :].rearrange("p (c i) t -> p c t i", i=4),
+                    z_planes[h][:, :, j0 + c0 : j0 + c0 + step].rearrange("p t (c i) -> p c t i", i=4),
+                )
             return z_bf
 
         def quantise(q, z_bf):
@@ -229,37 +230,41 @@ def tile_picked_ygcb_none_p_kernel(tc, x_words, x_scales, w1, w2, score, offs, o
                 stop=True,
             )
 
-        def finish(q, z_bf):
+        def finish(q, z_bf, b):
             j0, width = starts[q], PIECES[q]
             z_codes, z_scales = quantise(q, z_bf)
-            acc = bank(q, "acc%d" % q)
+            acc = bank(b, "acc%d" % q)
             for g in range(groups):
                 product(acc[:, g * width : (g + 1) * width], g, z_codes, z_scales)
-            if q == 0:
-                for g in range(groups):
-                    result = keep.tile([P, width], F32, name="result_first%d" % g)
-                    nc.scalar.copy(result[:], acc[:, g * width : (g + 1) * width])
-                    nc.sync.dma_start(out[g * P : (g + 1) * P, j0 : j0 + width], result[:])
-                return
             result = keep.tile([P, groups * width], F32, name="result%d" % q)
             nc.scalar.copy(result[:], acc[:, 0 : groups * width])
             rows = out.rearrange("(g p) j -> p g j", p=P)
             nc.sync.dma_start(rows[:, :, j0 : j0 + width], result[:].rearrange("p (g j) -> p g j", g=groups))
 
-        def finish_shared(q, z_bf):
+        def finish_apart(q, z_bf, banks, ways):
             j0, width = starts[q], PIECES[q]
             z_codes, z_scales = quantise(q, z_bf)
-            for g, (b, empty, queue) in enumerate(((q, nc.vector.tensor_copy, nc.sync), (LAST_BANK, nc.scalar.copy, nc.scalar))):
-                acc = bank(b, "acc_last%d" % g)
+            for g, (empty, queue) in enumerate(ways):
+                acc = bank(banks[g], "acc%d_%d" % (q, g))
                 product(acc[:, 0:width], g, z_codes, z_scales)
-                result = keep.tile([P, width], F32, name="result_last%d" % g)
+                result = keep.tile([P, width], F32, name="result%d_%d" % (q, g))
                 empty(result[:], acc[:, 0:width])
                 queue.dma_start(out[g * P : (g + 1) * P, j0 : j0 + width], result[:])
 
-        woven = [weave(0), weave(1), None, weave(3), weave(4)]
-        finish(0, woven[0])
-        finish(1, woven[1])
-        woven[2] = weave(2)
-        finish(3, woven[3])
-        finish(4, woven[4])
-        finish_shared(2, woven[2])
+        def woven_tile(pool, q, **place):
+            return pool.tile([P, PIECES[q], PACK], BF16, name="z_bf%d" % q, align_bytes=64, **place)
+
+        by_scalar = ((nc.scalar.copy, nc.sync), (nc.scalar.copy, nc.sync))
+        shared = ((nc.vector.tensor_copy, nc.sync), (nc.scalar.copy, nc.scalar))
+        quantise_w2(0, keep.tile([P, P], U32, name="w2_codes0", tag="weighted%d" % (PACK * halves - 2), align_bytes=64))
+        woven0 = weave(0, nc.vector.tensor_copy, P, woven_tile(keep, 0))
+        quantise_w2(1, reuse.tile([P, P], U32, name="w2_codes1", align_bytes=64, offset=AT_LAST_SUMS))
+        woven3 = weave(3, nc.scalar.copy, P, woven_tile(reuse, 3, offset=AT_EARLY))
+        woven4 = weave(4, nc.scalar.copy, P, woven_tile(keep, 4))
+        finish_apart(0, woven0, (0, 1), by_scalar)
+        woven1 = weave(1, nc.vector.tensor_copy, PIECES[1], woven_tile(keep, 1, tag="neg_max"))
+        finish(3, woven3, 2)
+        finish_apart(1, woven1, (3, 4), by_scalar)
+        woven2 = weave(2, nc.vector.tensor_copy, PIECES[2], woven_tile(reuse, 2, offset=AT_EARLY))
+        finish(4, woven4, 5)
+        finish_apart(2, woven2, (6, 7), shared)

from contextlib import ExitStack

import concourse.mybir as mybir

K, T, S, H, N = 512, 4096, 1024, 512, 256
P = 128
PACK = 4
BANK = 512
FLOPS = 2 * K * H * S + 2 * H * N * S
BYTES = T * P * 4 + 16 * T + 4 * K * H + 4 * H * N + 4 * T + 2 * P * (S // 16) + 4 * N * S

F32 = mybir.dt.float32
BF16 = mybir.dt.bfloat16
I32 = mybir.dt.int32
U32 = mybir.dt.uint32
U16 = mybir.dt.uint16
U8 = mybir.dt.uint8
FP8X4 = mybir.dt.float8_e4m3fn_x4
ALU = mybir.AluOpType
ACT = mybir.ActivationFunctionType

SCORE_ROW = P - 1
SCALE_ROW = 48
SCORE_PIECE = 256
VECTOR_RUNS = (6, 10)
PLANE_BYTES = 2 * P * PACK
PIECES = (256, 256, 256, 128, 128)
AT_LAST_SUMS = 3 * PLANE_BYTES
AT_EARLY = AT_LAST_SUMS + 4 * P
RUN = 8
ZERO_SPLIT = 3712


def tile_picked_ygcb_none_p_kernel(tc, x_words, x_scales, w1, w2, score, offs, out):
    nc = tc.nc
    halves = S // BANK
    blocks = S // P
    with ExitStack() as ctx:
        keep = ctx.enter_context(tc.tile_pool(name="keep", bufs=1))
        reuse = ctx.enter_context(tc.tile_pool(name="reuse", bufs=1))
        psum = ctx.enter_context(tc.psum_pool(name="psum", bufs=1))

        def bank(b, name):
            return psum.tile([P, BANK], F32, name=name, tag="bank%d" % b)

        score_table = keep.tile([P, T], F32, name="score_table", align_bytes=64)
        half_rows = score.rearrange("r c -> (r c)")[0 : 3 * T].rearrange("(a x) -> a x", a=2)[:, 0 : T // 2]
        nc.sync.dma_start(score_table[SCORE_ROW:P, :].rearrange("p (a x) -> p a x", a=2), half_rows.unsqueeze(0))
        offsets = keep.tile([P, S // 16], U16, name="offsets")
        nc.sync.dma_start(offsets[:], offs)
        scale_table = keep.tile([P, T // 4], I32, name="scale_table", align_bytes=64)
        nc.sync.dma_start(scale_table[SCALE_ROW : SCALE_ROW + 16, :], x_scales[0].bitcast(I32))
        word_table = keep.tile([P, T], U32, name="word_table", align_bytes=64)
        nc.sync.dma_start(word_table[:].bitcast(I32), x_words[0].rearrange("p n t -> p (n t)").bitcast(I32))
        w1_raw = keep.tile([P, PACK, H], F32, name="w1_raw", align_bytes=64)
        nc.sync.dma_start(w1_raw[:], w1.rearrange("(p j) c -> p j c", j=PACK))


        zero = keep.tile([P, 1], F32, name="zero")
        nc.gpsimd.memset(zero[:], 0.0)
        apart = keep.tile([P, P], I32, name="apart")
        nc.gpsimd.iota(apart[:], [[-1, P]], base=0, channel_multiplier=1)
        nc.vector.memset(score_table[0:SCORE_ROW, 0:ZERO_SPLIT], 0.0)
        nc.scalar.copy(score_table[0:SCORE_ROW, ZERO_SPLIT:T], zero[0:SCORE_ROW, :].to_broadcast([SCORE_ROW, T - ZERO_SPLIT]))
        ident = keep.tile([P, P], F32, name="ident")
        nc.vector.tensor_single_scalar(ident[:], apart[:], 0.0, ALU.is_equal)
        nc.vector.memset(scale_table[0:SCALE_ROW, :], 0)
        nc.vector.memset(scale_table[SCALE_ROW + 16 : P, :], 0)
        picked_scales = keep.tile([P, S], U8, name="picked_scales", align_bytes=64)
        nc.vector.memset(picked_scales[:].bitcast(I32), 0)
        minus_one = keep.tile([P, 1], F32, name="minus_one")
        nc.scalar.activation(minus_one[:], zero[:], ACT.Copy, bias=-1.0)

        per_bank = BANK // P
        cols16 = BANK // 16
        lists = [offsets[:, h * cols16 : (h + 1) * cols16] for h in range(halves)]
        turned = bank(6, "turned")
        for first in range(0, S, SCORE_PIECE):
            picked_score = keep.tile([P, SCORE_PIECE], F32, name="picked_score%d" % first, align_bytes=64)
            nc.scalar.activation(picked_score[:], score_table[:].indirect(offsets[:, first // 16 : (first + SCORE_PIECE) // 16]), ACT.Copy)
            for b in range(SCORE_PIECE // P):
                left = 2 * (blocks - 1 - (first // P + b))
                nc.tensor.transpose(turned[:, left : left + P], picked_score[:, b * P : (b + 1) * P], ident[:])

        apart_scales = keep.tile([P, S], U8, name="apart_scales", align_bytes=64)
        nc.vector.tensor_copy(apart_scales[:], scale_table[:].bitcast(U8).indirect(offsets[:]))
        for q in range(4):
            nc.sync.dma_start(picked_scales[32 * q : 32 * q + 4, :].bitcast(I32), apart_scales[SCALE_ROW + 4 * q : SCALE_ROW + 4 * q + 4, :].bitcast(I32))
        w2_raw = keep.tile([P, PACK, N], F32, name="w2_raw", tag="scale_table", align_bytes=64)
        w2_rows = w2.rearrange("(b u r e) c -> u b r (e c)", u=2, r=RUN, e=2)
        for u in range(2):
            nc.sync.dma_start(w2_raw[:, 2 * u : 2 * u + 2, :].rearrange("p e c -> p (e c)"), w2_rows[u])

        neg_room = reuse.tile([P, 32], F32, name="neg_room", align_bytes=64, offset=PLANE_BYTES - 64)
        neg_cols = neg_room[:, 0:blocks]
        neg_col_max = keep.tile([P, 1], F32, name="neg_col_max", align_bytes=64)
        max_row = bank(3, "max_row")
        nc.vector.tensor_scalar(neg_cols, turned[:, SCORE_ROW : SCORE_ROW + 2 * blocks : 2], -1.0, None, ALU.mult, ALU.min, accum_out=neg_col_max[:])
        nc.tensor.transpose(max_row[:, 0:P], neg_col_max[:].to_broadcast([P, P]), ident[:])
        spread = []
        for h in range(halves):
            sp = bank(4 + h, "spread%d" % h)
            for b in range(per_bank):
                c = blocks - 1 - (h * per_bank + b)
                nc.tensor.transpose(sp[:, b * P : (b + 1) * P], neg_cols[:, c : c + 1].to_broadcast([P, P]), ident[:])
            spread.append(sp)
        neg_row = keep.tile([P, P], F32, name="neg_row", align_bytes=64)
        neg_max = keep.tile([P, 1], F32, name="neg_max", align_bytes=64)
        words = keep.tile([P, S], U32, name="words", align_bytes=64)
        nc.vector.tensor_scalar(neg_row[:], max_row[:, 0:P], 1.0, None, ALU.mult, ALU.min, accum_out=neg_max[:])
        for h in range(halves):
            nc.vector.tensor_copy(words[:, h * BANK : (h + 1) * BANK], word_table[:].indirect(lists[h]))

        ee = keep.tile([P, S], F32, name="ee")
        part_total = keep.tile([P, halves], F32, name="part_total")
        for h in range(halves):
            nc.scalar.activation(ee[:, h * BANK : (h + 1) * BANK], spread[h][:], ACT.Exp, bias=neg_max[:], scale=-1.0, accum_out=part_total[:, h : h + 1])
        total = keep.tile([P, 1], F32, name="total")
        nc.gpsimd.tensor_tensor(total[:], part_total[:, 0:1], part_total[:, 1:2], ALU.add)
        inv_total = keep.tile([P, 1], F32, name="inv_total")
        nc.gpsimd.tensor_tensor(inv_total[:], total[:], minus_one[:], ALU.pow)

        columns = w1_raw[:].rearrange("p j (b u h i e) -> p u e b h j i", u=2, h=RUN // 2, i=2, e=2)

        def cast_plane(copy, t, plane, b0, b1):
            rows = plane.rearrange("p (b h i) j -> p b h j i", h=RUN // 2, i=2)
            copy(rows[:, b0:b1], columns[:, t // 2, t % 2, b0:b1])

        def quantise_plane(t, plane):
            codes = keep.tile([P, P], U32, name="w1_codes%d" % t, align_bytes=64)
            scales = keep.tile([P, P], U8, name="w1_scales%d" % t, align_bytes=64)
            nc.vector.quantize_mx(codes[:].bitcast(FP8X4), scales[:], plane.rearrange("p m j -> p (m j)"))
            return codes, scales

        plane0 = reuse.tile([P, P, PACK], BF16, name="plane0", align_bytes=64, offset=0)
        odd_planes = reuse.tile([P, 2, P, PACK], BF16, name="odd_planes", align_bytes=64, offset=PLANE_BYTES)
        runs = P // RUN
        for t, plane in ((0, plane0[:]), (1, odd_planes[:, 0])):
            cast_plane(nc.vector.tensor_copy, t, plane, 0, VECTOR_RUNS[t])
            cast_plane(nc.scalar.copy, t, plane, VECTOR_RUNS[t], runs)
        cast_plane(nc.scalar.copy, 3, odd_planes[:, 1], 0, runs)
        w1_mx = {0: quantise_plane(0, plane0[:]), 1: quantise_plane(1, odd_planes[:, 0])}
        plane2 = reuse.tile([P, P, PACK], BF16, name="plane2", align_bytes=64, offset=0)
        cast_plane(nc.vector.tensor_copy, 2, plane2[:], 0, runs)
        w1_mx[3] = quantise_plane(3, odd_planes[:, 1])
        w1_mx[2] = quantise_plane(2, plane2[:])
        w1_codes = [w1_mx[t][0] for t in range(PACK)]
        w1_scales = [w1_mx[t][1] for t in range(PACK)]

        w2_bf = keep.tile([P, N, PACK], BF16, name="w2_bf", tag="neg_max", align_bytes=64)
        nc.scalar.copy(
            w2_bf[:].rearrange("p (c i) j -> p c j i", i=4),
            w2_raw[:].rearrange("p j (c i) -> p c j i", i=4),
        )

        starts = [sum(PIECES[:q]) for q in range(len(PIECES))]
        z_planes = [
            keep.tile([P, PACK, BANK], BF16, name="z_planes0", tag="scale_table", align_bytes=64),
            keep.tile([P, PACK, BANK], BF16, name="z_planes1", tag="w1_raw", align_bytes=64),
        ]
        for t in range(PACK):
            y = []
            if t < PACK - 1:
                part_ctx = keep.tile([P, halves], F32, name="part_ctx%d" % t)
            else:
                part_ctx = reuse.tile([P, halves], F32, name="part_ctx%d" % t, align_bytes=64, offset=AT_LAST_SUMS)
            for h in range(halves):
                js = slice(h * BANK, (h + 1) * BANK)
                u = t * halves + h
                yb = bank(u, "y%d" % u)
                nc.tensor.matmul_mx(
                    yb[:],
                    lhsT=w1_codes[t][:].bitcast(FP8X4),
                    lhsT_scale=w1_scales[t][:],
                    rhs=words[:, js].bitcast(FP8X4),
                    rhs_scale=picked_scales[:, js],
                    start=True,
                    stop=True,
                )
                weighted = keep.tile([P, BANK], F32, name="weighted%d" % u, tag="weighted%d" % u, align_bytes=64)
                nc.vector.scalar_tensor_tensor(weighted[:], yb[:], inv_total[:], ee[:, js], ALU.mult, ALU.mult, accum_out=part_ctx[:, h : h + 1])
                y.append(yb)
            context = keep.tile([P, 1], F32, name="context%d" % t)
            first, second = part_ctx[:, 0:1], part_ctx[:, 1:2]
            nc.gpsimd.tensor_tensor(context[:], first, second, ALU.add)
            if t < PACK - 1:
                cuts = [0, BANK, S]
            else:
                for c0 in range(0, PIECES[0], P):
                    nc.vector.tensor_scalar(z_planes[0][:, t, c0 : c0 + P], y[0][:, c0 : c0 + P], first, second, ALU.add, ALU.add)
                cuts = [PIECES[0], BANK, S]
            for c0, c1 in zip(cuts, cuts[1:]):
                h = c0 // BANK
                nc.scalar.activation(z_planes[h][:, t, c0 - h * BANK : c1 - h * BANK], y[h][:, c0 - h * BANK : c1 - h * BANK], ACT.Identity, bias=context[:])

        w2_codes, w2_scales = [], []

        def quantise_w2(g, codes):
            scales = keep.tile([P, P], U8, name="w2_scales%d" % g, align_bytes=64)
            nc.vector.quantize_mx(codes[:].bitcast(FP8X4), scales[:], w2_bf[:, g * P : (g + 1) * P, :].rearrange("p c j -> p (c j)"))
            w2_codes.append(codes)
            w2_scales.append(scales)

        groups = N // P

        def weave(q, copy, step, z_bf):
            h, j0 = divmod(starts[q], BANK)
            for c0 in range(0, PIECES[q], step):
                copy(
                    z_bf[:, c0 : c0 + step, :].rearrange("p (c i) t -> p c t i", i=4),
                    z_planes[h][:, :, j0 + c0 : j0 + c0 + step].rearrange("p t (c i) -> p c t i", i=4),
                )
            return z_bf

        def quantise(q, z_bf):
            width = PIECES[q]
            z_codes = keep.tile([P, width], U32, name="z_codes%d" % q, align_bytes=64)
            z_scales = keep.tile([P, width], U8, name="z_scales%d" % q, align_bytes=64)
            nc.vector.quantize_mx(z_codes[:].bitcast(FP8X4), z_scales[:], z_bf[:].rearrange("p c t -> p (c t)"))
            return z_codes, z_scales

        def product(acc, g, z_codes, z_scales):
            nc.tensor.matmul_mx(
                acc,
                lhsT=w2_codes[g][:].bitcast(FP8X4),
                lhsT_scale=w2_scales[g][:],
                rhs=z_codes[:].bitcast(FP8X4),
                rhs_scale=z_scales[:],
                start=True,
                stop=True,
            )

        def finish(q, z_bf, b):
            j0, width = starts[q], PIECES[q]
            z_codes, z_scales = quantise(q, z_bf)
            acc = bank(b, "acc%d" % q)
            for g in range(groups):
                product(acc[:, g * width : (g + 1) * width], g, z_codes, z_scales)
            result = keep.tile([P, groups * width], F32, name="result%d" % q)
            nc.scalar.copy(result[:], acc[:, 0 : groups * width])
            rows = out.rearrange("(g p) j -> p g j", p=P)
            nc.sync.dma_start(rows[:, :, j0 : j0 + width], result[:].rearrange("p (g j) -> p g j", g=groups))

        def finish_apart(q, z_bf, banks, ways):
            j0, width = starts[q], PIECES[q]
            z_codes, z_scales = quantise(q, z_bf)
            for g, (empty, queue) in enumerate(ways):
                acc = bank(banks[g], "acc%d_%d" % (q, g))
                product(acc[:, 0:width], g, z_codes, z_scales)
                result = keep.tile([P, width], F32, name="result%d_%d" % (q, g))
                empty(result[:], acc[:, 0:width])
                queue.dma_start(out[g * P : (g + 1) * P, j0 : j0 + width], result[:])

        def woven_tile(pool, q, **place):
            return pool.tile([P, PIECES[q], PACK], BF16, name="z_bf%d" % q, align_bytes=64, **place)

        by_scalar = ((nc.scalar.copy, nc.sync), (nc.scalar.copy, nc.sync))
        shared = ((nc.vector.tensor_copy, nc.sync), (nc.scalar.copy, nc.scalar))
        quantise_w2(0, keep.tile([P, P], U32, name="w2_codes0", tag="weighted%d" % (PACK * halves - 2), align_bytes=64))
        woven0 = weave(0, nc.vector.tensor_copy, P, woven_tile(keep, 0))
        quantise_w2(1, reuse.tile([P, P], U32, name="w2_codes1", align_bytes=64, offset=AT_LAST_SUMS))
        woven3 = weave(3, nc.scalar.copy, P, woven_tile(reuse, 3, offset=AT_EARLY))
        woven4 = weave(4, nc.scalar.copy, P, woven_tile(keep, 4))
        finish_apart(0, woven0, (0, 1), by_scalar)
        woven1 = weave(1, nc.vector.tensor_copy, PIECES[1], woven_tile(keep, 1, tag="neg_max"))
        finish(3, woven3, 2)
        finish_apart(1, woven1, (3, 4), by_scalar)
        woven2 = weave(2, nc.vector.tensor_copy, PIECES[2], woven_tile(reuse, 2, offset=AT_EARLY))
        finish(4, woven4, 5)
        finish_apart(2, woven2, (6, 7), shared)
